import numpy as np
import ml_dtypes


def mxq(x, axis, fmt="e4m3"):
    dtype, down = {"e4m3": (ml_dtypes.float8_e4m3fn, 7), "e5m2": (ml_dtypes.float8_e5m2, 14)}[fmt]
    v = np.moveaxis(np.asarray(x, np.float32).astype(ml_dtypes.bfloat16).astype(np.float64), axis, -1)
    blocks = v.reshape(v.shape[:-1] + (-1, 32))
    amax = np.abs(blocks).max(-1, keepdims=True)
    byte = np.maximum(np.where(amax > 0, np.frexp(amax)[1] - 1 + 127, 0) - down, 1)
    scale = np.exp2(byte - 127.0)
    codes = (blocks / scale).astype(np.float32).astype(dtype).astype(np.float64)
    return np.moveaxis((codes * scale).reshape(v.shape), -1, axis)


WIDE = False


def mx_kscale(k):
    if not WIDE:
        return np.ones(k)
    levels = np.array([10, -10, 5, -5, 0])
    if k % 512:
        return np.exp2(np.random.permutation(np.resize(levels, k // 32))).repeat(32)
    a = np.empty((k // 512, 16))
    for p in range(k // 512):
        a[p, :8] = np.random.permutation(np.resize(levels, 8))
        for g in range(8):
            far = levels[np.abs(levels - a[p, g]) >= 10]
            a[p, g + 8] = far[np.random.randint(len(far))]
    return np.exp2(a.ravel()).repeat(32)


BF16 = ml_dtypes.bfloat16


def bf(x):
    return np.asarray(x, np.float32).astype(BF16)


def f64(x):
    return np.asarray(x).astype(np.float64)


E2M1 = np.array([0.0, 0.5, 1.0, 1.5, 2.0, 3.0, 4.0, 6.0, -0.0, -0.5, -1.0, -1.5, -2.0, -3.0, -4.0, -6.0])


def pack_weight(w, fmt):
    k, n = w.shape
    w = f64(bf(w)).reshape(k // 32, 32, n)
    amax = np.abs(w).max(1)
    if fmt == "e4m3":
        byte = np.frexp(amax)[1] - 1 + 127 - 7
    else:
        mant, ex = np.frexp(amax / 6.0)
        byte = np.where(mant > 0.5, ex, ex - 1) + 127
    byte = np.clip(np.where(amax > 0, byte, 1), 1, 254)
    scaled = (w * np.exp2(127.0 - byte)[:, None, :]).reshape(k, n).astype(np.float32)
    by_word = np.ascontiguousarray(scaled.reshape(k // 512, 128, 4, n).transpose(0, 1, 3, 2))
    if fmt == "e4m3":
        words = by_word.astype(ml_dtypes.float8_e4m3fn).view(np.uint8)
    else:
        c = by_word.astype(ml_dtypes.float4_e2m1fn).view(np.uint8) & 0xF
        words = c[..., 0::2] | (c[..., 1::2] << 4)
    return np.ascontiguousarray(words), np.ascontiguousarray(byte.astype(np.uint8).reshape(k // 512, 16, n))


def unpack_weight(words, scales, fmt):
    g, p, n, _ = words.shape
    if fmt == "e4m3":
        vals = np.ascontiguousarray(words).view(ml_dtypes.float8_e4m3fn).astype(np.float64)
    else:
        nib = np.empty((g, p, n, 4), np.uint8)
        nib[..., 0::2] = words & 0xF
        nib[..., 1::2] = words >> 4
        vals = E2M1[nib]
    vals = vals * np.repeat(np.exp2(scales.astype(np.float64) - 127.0), 8, axis=1)[..., None]
    return vals.transpose(0, 1, 3, 2).reshape(g * 512, n)
def pack4(w):
    words, scales = pack_weight(w, "e2m1")
    return words.reshape(words.shape[0], 128, -1), scales


def unpack4(words, scales):
    return unpack_weight(words.reshape(words.shape[0], 128, -1, 2), scales, "e2m1")


E4M3FN = np.array([(-1.0 if i & 128 else 1.0) * ((1.0 + (i & 7) / 8.0) * 2.0 ** (((i >> 3) & 15) - 7) if i & 120 else (i & 7) * 2.0 ** -9) for i in range(256)])


def e4m3fn_bytes(y):
    return np.clip(np.asarray(y, np.float64), -448.0, 448.0).astype(np.float32).astype(ml_dtypes.float8_e4m3fn).view(np.uint8)


def e4m3fn_values(b):
    return E4M3FN[b]


V, B, D, H, O = 2, 512, 512, 512, 512
C = 2 * H


def sigmoid(v):
    return 1.0 / (1.0 + np.exp(-v))


def project(xi, weight, bias):
    return sigmoid((xi @ weight) + bias) - 0.5


def draw0():
    s, t = mx_kscale(D), mx_kscale(C)
    x = bf(np.random.standard_normal((V, B, D)) * s)
    p = bf(np.random.standard_normal((V, D, H)) / np.sqrt(D) / s[:, None])
    b = bf(np.random.standard_normal((V, H)) * 0.3)
    g = bf((1.0 + 0.1 * np.random.standard_normal(C)) * t)
    wd_words, wd_scales = pack4(np.random.standard_normal((C, O)) * 4.0 / np.sqrt(C) / t[:, None])
    bd = bf(np.random.standard_normal(O) * 0.3)
    return {"x": x,
            "p": p,
            "b": b,
            "g": g,
            "wd_words": wd_words,
            "wd_scales": wd_scales,
            "bd": bd}


def core(x, p, b, g, wd_words, wd_scales, bd):
    xq = mxq(f64(x), 2, "e4m3")
    pq = mxq(f64(p), 1, "e4m3")
    bias, gain = f64(b), f64(g)
    m_0 = project(xq[0], pq[0], bias[0])
    m_1 = project(xq[1], pq[0], bias[0])
    s_0 = project(xq[0], pq[1], bias[1])
    s_1 = project(xq[1], pq[1], bias[1])
    c_0 = np.concatenate([m_0, s_0], axis=-1)
    c_1 = np.concatenate([m_1, s_1], axis=-1)
    q = mxq(np.stack([c_0, c_1], axis=0) * gain, 2, "e4m3")
    q_2 = np.concatenate([q[1][:, :H], q[0][:, H:]], axis=-1)
    q_3 = np.concatenate([q[0][:, :H], q[1][:, H:]], axis=-1)
    cq = np.stack([q[0], q[1], q_2, q_3], axis=0)
    return sigmoid((cq @ unpack4(wd_words, wd_scales)) + f64(bd))


def setup_inputs():
    drawn = draw0()
    full = np.asarray(drawn['x']).astype(np.float64)
    scale = (np.abs(full).reshape(2, 4, 128, 4, 128).max(axis=(2, 4)) / 448.0).astype(np.float32)
    given = {}
    for key, value in drawn.items():
        if key == 'x':
            given['x_bytes'] = e4m3fn_bytes(full / np.repeat(np.repeat(scale.astype(np.float64), 128, axis=1), 128, axis=2))
            given['x_scale'] = scale
        else:
            given[key] = value
    return given


def reference(x_bytes, x_scale, p, b, g, wd_words, wd_scales, bd):
    return core(e4m3fn_values(x_bytes) * np.repeat(np.repeat(x_scale.astype(np.float64), 128, axis=1), 128, axis=2), p, b, g, wd_words, wd_scales, bd)

@@ -1,0 +1,375 @@
+from contextlib import ExitStack
+
+import concourse.mybir as mybir
+from concourse.masks import make_identity
+
+F32 = mybir.dt.float32
+BF16 = mybir.dt.bfloat16
+I32 = mybir.dt.int32
+U32 = mybir.dt.uint32
+U8 = mybir.dt.uint8
+FP8 = mybir.dt.float8_e4m3fn
+FP8X4 = mybir.dt.float8_e4m3fn_x4
+FP4X4 = mybir.dt.float4_e2m1fn_x4
+ACT = mybir.ActivationFunctionType
+MULT = mybir.AluOpType.mult
+ADD = mybir.AluOpType.add
+
+P = 128
+T4 = 4
+V = 2
+B = 512
+D = 512
+H = 512
+O = 512
+PARTS = ((0, 0), (1, 1), (1, 0), (0, 1))
+
+FLOPS = 2 * (V * V * B * D * H + len(PARTS) * B * 2 * H * O)
+
+
+def tile_switchtabmutualsalientswap_d2p_kernel(tc, x_bytes, x_scale, p, b, g, wd_words, wd_scales, bd, out):
+    nc = tc.nc
+    with ExitStack() as ctx:
+        keep = ctx.enter_context(tc.tile_pool(name="keep", bufs=1))
+        wide = ctx.enter_context(tc.tile_pool(name="wide", bufs=4))
+        work = ctx.enter_context(tc.tile_pool(name="work", bufs=2))
+        outs = ctx.enter_context(tc.tile_pool(name="outs", bufs=4))
+        ps1 = ctx.enter_context(tc.psum_pool(name="ps1", bufs=4))
+        ps2 = ctx.enter_context(tc.psum_pool(name="ps2", bufs=4))
+        ctx.enter_context(tc.manual_schedule())
+
+        def kept(shape, dtype, label):
+            made = keep.tile(shape, dtype, name=label, align_bytes=64)
+            return made
+
+        xs = kept([P, V * 16], F32, "xs")
+        nc.scalar.dma_start(out=xs[:], in_=x_scale.rearrange("a i j -> (a i j)").partition_broadcast(P))
+        braw = kept([P, V, T4], BF16, "braw")
+        nc.scalar.dma_start(out=braw[:], in_=b.rearrange("a (q t) -> q a t", t=T4))
+        graw = kept([P, 2, T4], BF16, "graw")
+        nc.scalar.dma_start(out=graw[:], in_=g.rearrange("(a q t) -> q a t", a=2, t=T4))
+
+        ident = kept([P, P], F32, "ident")
+        make_identity(nc, ident[:])
+        warm = kept([P, 1], F32, "warm")
+        nc.vector.memset(warm[:], 0.0)
+        warmed = kept([P, 1], F32, "warmed")
+        nc.scalar.activation(out=warmed[:], in_=warm[:], func=ACT.Sigmoid)
+        wds = kept([P, 2, O], U8, "wds")
+        nc.vector.memset(wds[:].rearrange("q g n -> q (g n)").bitcast(I32), 0)
+        identb = kept([P, P], BF16, "identb")
+        nc.vector.tensor_copy(out=identb[:], in_=ident[:])
+
+        xb = {}
+
+        def load_x(a, h):
+            tile = kept([P, 2, D], U8, "xb%d%d" % (a, h))
+            nc.sync.dma_start(out=tile[:], in_=x_bytes[a, 256 * h : 256 * (h + 1), :].rearrange("(i q) k -> q i k", q=P))
+            xb[a, h] = tile
+
+        praw = {}
+
+        def load_p(w):
+            tile = kept([P, T4, H], BF16, "praw%d" % w)
+            nc.sync.dma_start(out=tile[:], in_=p[w].rearrange("(q j) c -> q j c", j=T4))
+            praw[w] = tile
+
+        load_x(0, 0)
+        load_x(0, 1)
+        load_p(0)
+        load_p(1)
+        load_x(1, 0)
+        load_x(1, 1)
+        wdw = kept([P, 2, 2 * O], U8, "wdw")
+        nc.sync.dma_start(out=wdw[:].bitcast(I32), in_=wd_words.bitcast(I32).rearrange("g q n -> q g n"))
+        for quad in range(4):
+            nc.sync.dma_start(
+                out=wds[32 * quad : 32 * quad + 4, :, :].bitcast(I32),
+                in_=wd_scales[:, 4 * quad : 4 * quad + 4, :].bitcast(I32).rearrange("g q n -> q g n"),
+            )
+        bdt = kept([P, O], BF16, "bdt")
+        nc.sync.dma_start(out=bdt[:], in_=bd.partition_broadcast(P))
+
+        bh = kept([P, V * T4], F32, "bh")
+        nc.gpsimd.tensor_scalar(out=bh[:], in0=braw[:].rearrange("q a t -> q (a t)"), scalar1=0.5, scalar2=0.0, op0=MULT, op1=ADD)
+        gh = kept([P, 2 * T4], F32, "gh")
+        nc.gpsimd.tensor_scalar(out=gh[:], in0=graw[:].rearrange("q a t -> q (a t)"), scalar1=0.5, scalar2=0.0, op0=MULT, op1=ADD)
+
+        xw = {}
+        xg = {}
+        xc = {}
+        xsc = {}
+        pg = {}
+        pc = {}
+        psc = {}
+        for a in range(V):
+            xg[a] = kept([P, B, T4], BF16, "xg%d" % a)
+            xc[a] = kept([P, B], U32, "xc%d" % a)
+            xsc[a] = kept([P, B], U8, "xsc%d" % a)
+            pg[a] = kept([P, T4 * P * T4], BF16, "pg%d" % a)
+            pc[a] = kept([P, H], U32, "pc%d" % a)
+            psc[a] = kept([P, H], U8, "psc%d" % a)
+            for h in range(2):
+                xw[a, h] = kept([P, 2, D], BF16, "xw%d%d" % (a, h))
+        qc = {}
+        qs = {}
+        for a in range(V):
+            for w in range(2):
+                qc[a, w] = kept([P, B], U32, "qc%d%d" % (a, w))
+                qs[a, w] = kept([P, B], U8, "qs%d%d" % (a, w))
+
+        def widen(a, h, i, engine):
+            for j in range(4):
+                cols = slice(P * j, P * (j + 1))
+                at = 16 * a + 4 * (2 * h + i) + j
+                src = xb[a, h][:, i, cols].bitcast(FP8)
+                dst = xw[a, h][:, i, cols]
+                if engine == "v":
+                    nc.vector.tensor_scalar(out=dst, in0=src, scalar1=xs[:, at : at + 1], scalar2=None, op0=MULT)
+                else:
+                    nc.scalar.activation(out=dst, in_=src, func=ACT.Copy, scale=xs[:, at : at + 1])
+
+        turned = {}
+
+        def turn(a, h):
+            bank = ps2.tile([P, 2, 2, P], F32, name="bank2")
+            for i in range(2):
+                words = xw[a, h][:, i, :].bitcast(F32)
+                for u in range(2):
+                    nc.tensor.transpose(bank[:, i, u, :], words[:, u : D // 2 : 2], ident[:])
+            turned[a, h] = bank
+
+        def empty(a, h, engine):
+            words = xg[a][:].rearrange("q n t -> q (n t)").bitcast(F32)
+            dst = words[:, 512 * h : 512 * (h + 1)].rearrange("q (i r u) -> q i r u", i=2, u=2)
+            src = turned[a, h][:].rearrange("q i u r -> q i r u")
+            if engine == "v":
+                nc.vector.tensor_copy(out=dst, in_=src)
+            else:
+                nc.scalar.copy(out=dst, in_=src)
+
+        def quant_x(a, h0, h1):
+            cols = slice(256 * h0, 256 * h1)
+            nc.vector.quantize_mx(
+                out=xc[a][:, cols].bitcast(FP8X4),
+                scales=xsc[a][:, cols],
+                in_=xg[a][:].rearrange("q n t -> q (n t)")[:, 1024 * h0 : 1024 * h1],
+            )
+
+        def interleave(w, t0, t1, engine):
+            dst = pg[w][:].rearrange("q (t m j) -> q t m j", t=T4, j=T4)[:, t0:t1]
+            src = praw[w][:].rearrange("q j (m t) -> q t m j", t=T4)[:, t0:t1]
+            if engine == "v":
+                nc.vector.tensor_copy(out=dst, in_=src)
+            else:
+                nc.scalar.copy(out=dst, in_=src)
+
+        def quant_p(w, t0, t1):
+            cols = slice(P * t0, P * t1)
+            nc.vector.quantize_mx(
+                out=pc[w][:, cols].bitcast(FP8X4), scales=psc[w][:, cols], in_=pg[w][:, T4 * P * t0 : T4 * P * t1]
+            )
+
+        th = {}
+
+        def project(a, w, t, h0=0, h1=2):
+            if t == 0 and h0 == 0:
+                parts = wide.tile([P, T4, B], F32, name="th")
+                th[a, w] = parts
+            rows = slice(256 * h0, 256 * h1)
+            acc = ps1.tile([P, B], F32, name="bank1")
+            cols = slice(P * t, P * (t + 1))
+            nc.tensor.matmul_mx(
+                out=acc[:, 0 : 256 * (h1 - h0)],
+                lhsT=pc[w][:, cols].bitcast(FP8X4),
+                lhsT_scale=psc[w][:, cols],
+                rhs=xc[a][:, rows].bitcast(FP8X4),
+                rhs_scale=xsc[a][:, rows],
+                start=True,
+                stop=True,
+            )
+            at = T4 * w + t
+            nc.scalar.activation(
+                out=th[a, w][:, t, rows],
+                in_=acc[:, 0 : 256 * (h1 - h0)],
+                func=ACT.Tanh,
+                bias=bh[:, at : at + 1],
+                scale=0.5,
+            )
+
+        qg = {}
+
+        def gain(a, w, h):
+            if h == 0:
+                made = work.tile([P, B, T4], BF16, name="qg", align_bytes=64)
+                qg[a, w] = made
+            rows = slice(256 * h, 256 * (h + 1))
+            nc.vector.tensor_tensor(
+                out=qg[a, w][:, rows, :].rearrange("q (c i) t -> q c t i", i=4),
+                in0=th[a, w][:, :, rows].rearrange("q t (c i) -> q c t i", i=4),
+                in1=gh[:, T4 * w : T4 * (w + 1)].unsqueeze(1).unsqueeze(3).to_broadcast([P, 64, T4, 4]),
+                op=MULT,
+            )
+
+        def quant_q(a, w, h0, h1):
+            cols = slice(256 * h0, 256 * h1)
+            nc.vector.quantize_mx(
+                out=qc[a, w][:, cols].bitcast(FP8X4),
+                scales=qs[a, w][:, cols],
+                in_=qg[a, w][:].rearrange("q n t -> q (n t)")[:, 1024 * h0 : 1024 * h1],
+            )
+
+        zs = {}
+
+        def decode(j, i, slot):
+            if slot == 0:
+                made = outs.tile([P, 2, O], F32, name="z")
+                zs[j] = made
+            if j in (1, 3) and slot == 1:
+                acc = ps1.tile([P, O], F32, name="bank1")
+            else:
+                acc = ps2.tile([P, O], F32, name="bank2")
+            cols = slice(P * i, P * (i + 1))
+            for w in range(2):
+                a = PARTS[j][w]
+                nc.tensor.matmul_mx(
+                    out=acc[:],
+                    lhsT=qc[a, w][:, cols].bitcast(FP8X4),
+                    lhsT_scale=qs[a, w][:, cols],
+                    rhs=wdw[:, w, :].bitcast(FP4X4),
+                    rhs_scale=wds[:, w, :],
+                    start=(w == 0),
+                    stop=(w == 1),
+                )
+            nc.vector.tensor_tensor(out=zs[j][:, slot, :], in0=acc[:], in1=bdt[:], op=ADD)
+
+        bdc = kept([P, 4], F32, "bdc")
+
+        def bias_columns():
+            bank = ps2.tile([P, 4, P], BF16, name="bank2")
+            for c in range(4):
+                nc.tensor.transpose(bank[:, c, :], bdt[:, P * c : P * (c + 1)], identb[:])
+            turned["bd"] = bank
+
+        def bias_copy():
+            nc.vector.tensor_copy(out=bdc[:].unsqueeze(2), in_=turned["bd"][:, :, 0:1])
+
+        yt = {}
+
+        def decode_t(j):
+            made = outs.tile([P, 4, B], F32, name="yt", bufs=1)
+            yt[j] = made
+            for c in range(4):
+                acc = ps2.tile([P, B], F32, name="bank2")
+                for w in range(2):
+                    a = PARTS[j][w]
+                    nc.tensor.matmul_mx(
+                        out=acc[:],
+                        lhsT=wdw[:, w, 2 * P * c : 2 * P * (c + 1)].bitcast(FP4X4),
+                        lhsT_scale=wds[:, w, P * c : P * (c + 1)],
+                        rhs=qc[a, w][:].bitcast(FP8X4),
+                        rhs_scale=qs[a, w][:],
+                        start=(w == 0),
+                        stop=(w == 1),
+                    )
+                nc.scalar.activation(out=yt[j][:, c, :], in_=acc[:], func=ACT.Sigmoid, bias=bdc[:, c : c + 1])
+
+        ys = {}
+
+        def flip(j, i):
+            bank = ps2.tile([P, O], F32, name="bank2")
+            for c in range(4):
+                nc.tensor.transpose(bank[:, P * c : P * (c + 1)], yt[j][:, c, P * i : P * (i + 1)], ident[:])
+            if i % 2 == 0:
+                made = outs.tile([P, 2, O], F32, name="y")
+                ys[j] = made
+            nc.scalar.copy(out=ys[j][:, i % 2, :], in_=bank[:])
+            if i % 2 == 1:
+                store(ys[j], j, i - 1, 2)
+
+        def store(tile, j, i0, count):
+            nc.sync.dma_start(
+                out=out[j, P * i0 : P * (i0 + count), :].rearrange("(i q) o -> q i o", q=P), in_=tile[:, 0:count, :]
+            )
+
+        def finish(j, i0, count, slot):
+            y = outs.tile([P, 2, O], F32, name="y")
+            nc.scalar.activation(out=y[:, 0:count, :], in_=zs[j][:, slot : slot + count, :], func=ACT.Sigmoid)
+            store(y, j, i0, count)
+
+        widen(0, 0, 0, "v")
+        widen(0, 0, 1, "v")
+        turn(0, 0)
+        widen(0, 1, 0, "v")
+        widen(0, 1, 1, "v")
+        turn(0, 1)
+        empty(0, 0, "s")
+        empty(0, 1, "s")
+        interleave(0, 0, 2, "v")
+        interleave(0, 2, 4, "s")
+        quant_x(0, 0, 1)
+        quant_p(0, 0, 2)
+        quant_x(0, 1, 2)
+        quant_p(0, 2, 4)
+        for t in range(4):
+            project(0, 0, t, 0, 1)
+        interleave(1, 2, 4, "s")
+        for t in range(4):
+            project(0, 0, t, 1, 2)
+        interleave(1, 0, 2, "v")
+        widen(1, 0, 0, "v")
+        widen(1, 0, 1, "v")
+        gain(0, 0, 0)
+        quant_p(1, 0, 2)
+        quant_p(1, 2, 4)
+        for t in range(4):
+            project(0, 1, t, 0, 1)
+        turn(1, 0)
+        widen(1, 1, 0, "v")
+        widen(1, 1, 1, "v")
+        turn(1, 1)
+        gain(0, 0, 1)
+        empty(1, 0, "s")
+        empty(1, 1, "s")
+        for t in range(4):
+            project(0, 1, t, 1, 2)
+        gain(0, 1, 0)
+        quant_x(1, 0, 2)
+        quant_q(0, 0, 0, 2)
+        bias_columns()
+        for w in range(2):
+            for t in range(4):
+                project(1, w, t)
+        gain(0, 1, 1)
+        bias_copy()
+        quant_q(0, 1, 0, 1)
+        quant_q(0, 1, 1, 2)
+        gain(1, 0, 0)
+        gain(1, 0, 1)
+        decode_t(0)
+        quant_q(1, 0, 0, 1)
+        quant_q(1, 0, 1, 2)
+        gain(1, 1, 0)
+        decode(2, 0, 0)
+        decode(2, 1, 1)
+        flip(0, 0)
+        flip(0, 1)
+        finish(2, 0, 2, 0)
+        gain(1, 1, 1)
+        quant_q(1, 1, 0, 1)
+        decode(2, 2, 0)
+        quant_q(1, 1, 1, 2)
+        decode(2, 3, 1)
+        flip(0, 2)
+        flip(0, 3)
+        finish(2, 2, 2, 0)
+        for i in (0, 2):
+            for j in (1, 3):
+                decode(j, i, 0)
+                if (i, j) == (2, 3):
+                    finish(j, i, 1, 0)
+                decode(j, i + 1, 1)
+                if (i, j) == (2, 3):
+                    finish(j, i + 1, 1, 1)
+                else:
+                    finish(j, i, 2, 0)

@@ -22,6 +22,8 @@ B = 512
 D = 512
 H = 512
 O = 512
+CHUNKS = B // P
+N = V * P
 PARTS = ((0, 0), (1, 1), (1, 0), (0, 1))
 
 FLOPS = 2 * (V * V * B * D * H + len(PARTS) * B * 2 * H * O)
@@ -31,41 +33,44 @@ def tile_switchtabmutualsalientswap_d2p_kernel(tc, x_bytes, x_scale, p, b, g, wd
     nc = tc.nc
     with ExitStack() as ctx:
         keep = ctx.enter_context(tc.tile_pool(name="keep", bufs=1))
-        wide = ctx.enter_context(tc.tile_pool(name="wide", bufs=4))
         work = ctx.enter_context(tc.tile_pool(name="work", bufs=2))
-        outs = ctx.enter_context(tc.tile_pool(name="outs", bufs=4))
-        ps1 = ctx.enter_context(tc.psum_pool(name="ps1", bufs=4))
-        ps2 = ctx.enter_context(tc.psum_pool(name="ps2", bufs=4))
+        ps_proj = ctx.enter_context(tc.psum_pool(name="ps_proj", bufs=3))
+        ps_dec = ctx.enter_context(tc.psum_pool(name="ps_dec", bufs=4))
+        ps_x = ctx.enter_context(tc.psum_pool(name="ps_x", bufs=1))
         ctx.enter_context(tc.manual_schedule())
 
         def kept(shape, dtype, label):
             made = keep.tile(shape, dtype, name=label, align_bytes=64)
             return made
 
-        xs = kept([P, V * 16], F32, "xs")
-        nc.scalar.dma_start(out=xs[:], in_=x_scale.rearrange("a i j -> (a i j)").partition_broadcast(P))
+        xs_rows = kept([P, V * CHUNKS], F32, "xs_rows")
+        nc.vector.memset(xs_rows[:], 0.0)
         braw = kept([P, V, T4], BF16, "braw")
-        nc.scalar.dma_start(out=braw[:], in_=b.rearrange("a (q t) -> q a t", t=T4))
         graw = kept([P, 2, T4], BF16, "graw")
-        nc.scalar.dma_start(out=graw[:], in_=g.rearrange("(a q t) -> q a t", a=2, t=T4))
 
-        ident = kept([P, P], F32, "ident")
-        make_identity(nc, ident[:])
         warm = kept([P, 1], F32, "warm")
         nc.vector.memset(warm[:], 0.0)
         warmed = kept([P, 1], F32, "warmed")
         nc.scalar.activation(out=warmed[:], in_=warm[:], func=ACT.Sigmoid)
+
+        ident = kept([P, P], F32, "ident")
+        make_identity(nc, ident[:])
+        identb = kept([P, P], BF16, "identb")
+        make_identity(nc, identb[:])
+        blocks = kept([P, P], F32, "blocks")
+        nc.vector.memset(blocks[:], 0.0)
+        for quad in range(4):
+            rows = slice(32 * quad, 32 * (quad + 1))
+            nc.vector.memset(blocks[rows, rows], 1.0)
         wds = kept([P, 2, O], U8, "wds")
         nc.vector.memset(wds[:].rearrange("q g n -> q (g n)").bitcast(I32), 0)
-        identb = kept([P, P], BF16, "identb")
-        nc.vector.tensor_copy(out=identb[:], in_=ident[:])
 
         xb = {}
 
-        def load_x(a, h):
-            tile = kept([P, 2, D], U8, "xb%d%d" % (a, h))
-            nc.sync.dma_start(out=tile[:], in_=x_bytes[a, 256 * h : 256 * (h + 1), :].rearrange("(i q) k -> q i k", q=P))
-            xb[a, h] = tile
+        def load_x(c):
+            tile = kept([P, V, D], U8, "xb%d" % c)
+            nc.sync.dma_start(out=tile[:], in_=x_bytes[:, P * c : P * (c + 1), :].rearrange("a q k -> q a k"))
+            xb[c] = tile
 
         praw = {}
 
@@ -74,12 +79,16 @@ def tile_switchtabmutualsalientswap_d2p_kernel(tc, x_bytes, x_scale, p, b, g, wd
             nc.sync.dma_start(out=tile[:], in_=p[w].rearrange("(q j) c -> q j c", j=T4))
             praw[w] = tile
 
-        load_x(0, 0)
-        load_x(0, 1)
+        load_x(0)
+        with nc.allow_non_contiguous_dma(reason="32 scales, turned on the way in"):
+            nc.sync.dma_start(out=xs_rows[0:P:32, :], in_=x_scale.rearrange("a i j -> j (a i)"))
         load_p(0)
+        nc.sync.dma_start(out=braw[:], in_=b.rearrange("a (q t) -> q a t", t=T4))
+        load_x(1)
         load_p(1)
-        load_x(1, 0)
-        load_x(1, 1)
+        nc.sync.dma_start(out=graw[:], in_=g.rearrange("(a q t) -> q a t", a=2, t=T4))
+        load_x(2)
+        load_x(3)
         wdw = kept([P, 2, 2 * O], U8, "wdw")
         nc.sync.dma_start(out=wdw[:].bitcast(I32), in_=wd_words.bitcast(I32).rearrange("g q n -> q g n"))
         for quad in range(4):
@@ -90,79 +99,91 @@ def tile_switchtabmutualsalientswap_d2p_kernel(tc, x_bytes, x_scale, p, b, g, wd
         bdt = kept([P, O], BF16, "bdt")
         nc.sync.dma_start(out=bdt[:], in_=bd.partition_broadcast(P))
 
+        xs = kept([P, V * CHUNKS], F32, "xs")
         bh = kept([P, V * T4], F32, "bh")
-        nc.gpsimd.tensor_scalar(out=bh[:], in0=braw[:].rearrange("q a t -> q (a t)"), scalar1=0.5, scalar2=0.0, op0=MULT, op1=ADD)
         gh = kept([P, 2 * T4], F32, "gh")
-        nc.gpsimd.tensor_scalar(out=gh[:], in0=graw[:].rearrange("q a t -> q (a t)"), scalar1=0.5, scalar2=0.0, op0=MULT, op1=ADD)
+        held = {}
+
+        def spread_scales():
+            bank = ps_dec.tile([P, V * CHUNKS], F32, name="dec")
+            nc.tensor.matmul(out=bank[:], lhsT=blocks[:], rhs=xs_rows[:], start=True, stop=True)
+            nc.scalar.copy(out=xs[:], in_=bank[:])
+
+        def halve(dst, src):
+            nc.scalar.activation(out=dst[:], in_=src[:].rearrange("q a t -> q (a t)"), func=ACT.Copy, scale=0.5)
 
         xw = {}
+
+        def widen(c, engine, a0=0, a1=V):
+            if a0 == 0:
+                made = work.tile([P, V * D], BF16, name="xw", align_bytes=64)
+                xw[c] = made
+            cols = slice(D * a0, D * a1)
+            src = xb[c][:].rearrange("q a k -> q (a k)")[:, cols].bitcast(FP8)
+            if engine == "v":
+                nc.vector.tensor_copy(out=xw[c][:, cols], in_=src)
+            else:
+                nc.scalar.copy(out=xw[c][:, cols], in_=src)
+
+        def turn(c, a0=0, a1=V, pool=ps_x, label="xt"):
+            bank = pool.tile([P, a1 - a0, 2, P], F32, name=label)
+            for a in range(a0, a1):
+                words = xw[c][:, D * a : D * (a + 1)].bitcast(F32)
+                for u in range(2):
+                    nc.tensor.transpose(bank[:, a - a0, u, :], words[:, u : D // 2 : 2], ident[:])
+                held["xt", c, a] = bank[:, a - a0, :, :]
+
         xg = {}
+
+        def scale_out(c, a, engine):
+            if c not in xg:
+                made = work.tile([P, V, P * T4], BF16, name="xg", align_bytes=64)
+                xg[c] = made
+            src = held["xt", c, a].bitcast(BF16).rearrange("q u (r e) -> q r u e", e=2)
+            dst = xg[c][:, a, :].rearrange("q (r u e) -> q r u e", u=2, e=2)
+            at = CHUNKS * a + c
+            if engine == "v":
+                nc.vector.tensor_scalar(out=dst, in0=src, scalar1=xs[:, at : at + 1], scalar2=None, op0=MULT)
+            else:
+                nc.scalar.activation(out=dst, in_=src, func=ACT.Copy, scale=xs[:, at : at + 1])
+
         xc = {}
         xsc = {}
+
+        def quant_x(c, a0=0, a1=V):
+            if a0 == 0:
+                xc[c] = kept([P, N], U32, "xc%d" % c)
+                xsc[c] = kept([P, N], U8, "xsc%d" % c)
+            cols = slice(P * a0, P * a1)
+            nc.vector.quantize_mx(
+                out=xc[c][:, cols].bitcast(FP8X4), scales=xsc[c][:, cols], in_=xg[c][:, a0:a1, :].rearrange("q a n -> q (a n)")
+            )
+
         pg = {}
         pc = {}
         psc = {}
-        for a in range(V):
-            xg[a] = kept([P, B, T4], BF16, "xg%d" % a)
-            xc[a] = kept([P, B], U32, "xc%d" % a)
-            xsc[a] = kept([P, B], U8, "xsc%d" % a)
-            pg[a] = kept([P, T4 * P * T4], BF16, "pg%d" % a)
-            pc[a] = kept([P, H], U32, "pc%d" % a)
-            psc[a] = kept([P, H], U8, "psc%d" % a)
-            for h in range(2):
-                xw[a, h] = kept([P, 2, D], BF16, "xw%d%d" % (a, h))
-        qc = {}
-        qs = {}
-        for a in range(V):
-            for w in range(2):
-                qc[a, w] = kept([P, B], U32, "qc%d%d" % (a, w))
-                qs[a, w] = kept([P, B], U8, "qs%d%d" % (a, w))
+        for w in range(2):
+            pg[w] = kept([P, T4 * P * T4], BF16, "pg%d" % w)
+            pc[w] = kept([P, H], U32, "pc%d" % w)
+            psc[w] = kept([P, H], U8, "psc%d" % w)
 
-        def widen(a, h, i, engine):
-            for j in range(4):
-                cols = slice(P * j, P * (j + 1))
-                at = 16 * a + 4 * (2 * h + i) + j
-                src = xb[a, h][:, i, cols].bitcast(FP8)
-                dst = xw[a, h][:, i, cols]
-                if engine == "v":
-                    nc.vector.tensor_scalar(out=dst, in0=src, scalar1=xs[:, at : at + 1], scalar2=None, op0=MULT)
-                else:
-                    nc.scalar.activation(out=dst, in_=src, func=ACT.Copy, scale=xs[:, at : at + 1])
-
-        turned = {}
-
-        def turn(a, h):
-            bank = ps2.tile([P, 2, 2, P], F32, name="bank2")
-            for i in range(2):
-                words = xw[a, h][:, i, :].bitcast(F32)
-                for u in range(2):
-                    nc.tensor.transpose(bank[:, i, u, :], words[:, u : D // 2 : 2], ident[:])
-            turned[a, h] = bank
-
-        def empty(a, h, engine):
-            words = xg[a][:].rearrange("q n t -> q (n t)").bitcast(F32)
-            dst = words[:, 512 * h : 512 * (h + 1)].rearrange("q (i r u) -> q i r u", i=2, u=2)
-            src = turned[a, h][:].rearrange("q i u r -> q i r u")
+        def lay_p(w, t0, engine, count=2):
+            dst = pg[w][:].rearrange("q (t m j) -> q t m j", t=T4, j=T4)[:, t0 : t0 + count]
+            src = praw[w][:].rearrange("q j (m t) -> q t m j", t=T4)[:, t0 : t0 + count]
             if engine == "v":
                 nc.vector.tensor_copy(out=dst, in_=src)
-            else:
+            elif engine == "s":
                 nc.scalar.copy(out=dst, in_=src)
+            else:
+                bank = ps_dec.tile([P, 2, P * T4], BF16, name="dec")
+                for t in range(2):
+                    nc.tensor.matmul(out=bank[:, t, :], lhsT=identb[:], rhs=src[:, t], start=True, stop=True)
+                held["pt", w, t0] = bank
 
-        def quant_x(a, h0, h1):
-            cols = slice(256 * h0, 256 * h1)
-            nc.vector.quantize_mx(
-                out=xc[a][:, cols].bitcast(FP8X4),
-                scales=xsc[a][:, cols],
-                in_=xg[a][:].rearrange("q n t -> q (n t)")[:, 1024 * h0 : 1024 * h1],
+        def empty_p(w, t0):
+            nc.scalar.copy(
+                out=pg[w][:, T4 * P * t0 : T4 * P * (t0 + 2)], in_=held["pt", w, t0][:].rearrange("q t n -> q (t n)")
             )
-
-        def interleave(w, t0, t1, engine):
-            dst = pg[w][:].rearrange("q (t m j) -> q t m j", t=T4, j=T4)[:, t0:t1]
-            src = praw[w][:].rearrange("q j (m t) -> q t m j", t=T4)[:, t0:t1]
-            if engine == "v":
-                nc.vector.tensor_copy(out=dst, in_=src)
-            else:
-                nc.scalar.copy(out=dst, in_=src)
 
         def quant_p(w, t0, t1):
             cols = slice(P * t0, P * t1)
@@ -172,204 +193,178 @@ def tile_switchtabmutualsalientswap_d2p_kernel(tc, x_bytes, x_scale, p, b, g, wd
 
         th = {}
 
-        def project(a, w, t, h0=0, h1=2):
-            if t == 0 and h0 == 0:
-                parts = wide.tile([P, T4, B], F32, name="th")
-                th[a, w] = parts
-            rows = slice(256 * h0, 256 * h1)
-            acc = ps1.tile([P, B], F32, name="bank1")
-            cols = slice(P * t, P * (t + 1))
-            nc.tensor.matmul_mx(
-                out=acc[:, 0 : 256 * (h1 - h0)],
-                lhsT=pc[w][:, cols].bitcast(FP8X4),
-                lhsT_scale=psc[w][:, cols],
-                rhs=xc[a][:, rows].bitcast(FP8X4),
-                rhs_scale=xsc[a][:, rows],
-                start=True,
-                stop=True,
-            )
-            at = T4 * w + t
-            nc.scalar.activation(
-                out=th[a, w][:, t, rows],
-                in_=acc[:, 0 : 256 * (h1 - h0)],
-                func=ACT.Tanh,
-                bias=bh[:, at : at + 1],
-                scale=0.5,
-            )
+        def project(c, w, t0):
+            acc = ps_proj.tile([P, 2, N], F32, name="proj")
+            for t in range(t0, t0 + 2):
+                cols = slice(P * t, P * (t + 1))
+                nc.tensor.matmul_mx(
+                    out=acc[:, t - t0, :],
+                    lhsT=pc[w][:, cols].bitcast(FP8X4),
+                    lhsT_scale=psc[w][:, cols],
+                    rhs=xc[c][:].bitcast(FP8X4),
+                    rhs_scale=xsc[c][:],
+                    start=True,
+                    stop=True,
+                )
+            held["proj", c, w, t0] = acc
+
+        def squash(c, w, t0):
+            if t0 == 0:
+                made = work.tile([P, T4, N], F32, name="th", bufs=4)
+                th[c, w] = made
+            acc = held["proj", c, w, t0]
+            for t in range(t0, t0 + 2):
+                at = T4 * w + t
+                nc.scalar.activation(
+                    out=th[c, w][:, t, :], in_=acc[:, t - t0, :], func=ACT.Tanh, bias=bh[:, at : at + 1], scale=0.5
+                )
 
         qg = {}
 
-        def gain(a, w, h):
-            if h == 0:
-                made = work.tile([P, B, T4], BF16, name="qg", align_bytes=64)
-                qg[a, w] = made
-            rows = slice(256 * h, 256 * (h + 1))
+        def gain(c, w):
+            if w == 0:
+                made = work.tile([P, 2, N * T4], BF16, name="qg", align_bytes=64)
+                qg[c] = made
             nc.vector.tensor_tensor(
-                out=qg[a, w][:, rows, :].rearrange("q (c i) t -> q c t i", i=4),
-                in0=th[a, w][:, :, rows].rearrange("q t (c i) -> q c t i", i=4),
-                in1=gh[:, T4 * w : T4 * (w + 1)].unsqueeze(1).unsqueeze(3).to_broadcast([P, 64, T4, 4]),
+                out=qg[c][:, w, :].rearrange("q (n i t) -> q n t i", i=4, t=T4),
+                in0=th[c, w][:].rearrange("q t (n i) -> q n t i", i=4),
+                in1=gh[:, T4 * w : T4 * (w + 1)].unsqueeze(1).unsqueeze(3).to_broadcast([P, N // 4, T4, 4]),
                 op=MULT,
             )
 
-        def quant_q(a, w, h0, h1):
-            cols = slice(256 * h0, 256 * h1)
+        qc = {}
+        qs = {}
+
+        def quant_q(c, w0, w1):
+            if w0 == 0:
+                codes = work.tile([P, 2 * N], U32, name="qc", align_bytes=64)
+                scales = work.tile([P, 2 * N], U8, name="qs", align_bytes=64)
+                qc[c] = codes
+                qs[c] = scales
+            cols = slice(N * w0, N * w1)
             nc.vector.quantize_mx(
-                out=qc[a, w][:, cols].bitcast(FP8X4),
-                scales=qs[a, w][:, cols],
-                in_=qg[a, w][:].rearrange("q n t -> q (n t)")[:, 1024 * h0 : 1024 * h1],
+                out=qc[c][:, cols].bitcast(FP8X4),
+                scales=qs[c][:, cols],
+                in_=qg[c][:, w0:w1, :].rearrange("q w n -> q (w n)"),
             )
 
-        zs = {}
-
-        def decode(j, i, slot):
-            if slot == 0:
-                made = outs.tile([P, 2, O], F32, name="z")
-                zs[j] = made
-            if j in (1, 3) and slot == 1:
-                acc = ps1.tile([P, O], F32, name="bank1")
-            else:
-                acc = ps2.tile([P, O], F32, name="bank2")
-            cols = slice(P * i, P * (i + 1))
-            for w in range(2):
-                a = PARTS[j][w]
+        def decode(c, j, w0=0, w1=2, pool=ps_dec, label="dec"):
+            if w0 == 0:
+                made = pool.tile([P, O], F32, name=label)
+                held["dec", c, j] = made
+            acc = held["dec", c, j]
+            for w in range(w0, w1):
+                at = N * w + P * PARTS[j][w]
                 nc.tensor.matmul_mx(
                     out=acc[:],
-                    lhsT=qc[a, w][:, cols].bitcast(FP8X4),
-                    lhsT_scale=qs[a, w][:, cols],
+                    lhsT=qc[c][:, at : at + P].bitcast(FP8X4),
+                    lhsT_scale=qs[c][:, at : at + P],
                     rhs=wdw[:, w, :].bitcast(FP4X4),
                     rhs_scale=wds[:, w, :],
                     start=(w == 0),
                     stop=(w == 1),
                 )
-            nc.vector.tensor_tensor(out=zs[j][:, slot, :], in0=acc[:], in1=bdt[:], op=ADD)
 
-        bdc = kept([P, 4], F32, "bdc")
+        zs = {}
 
-        def bias_columns():
-            bank = ps2.tile([P, 4, P], BF16, name="bank2")
-            for c in range(4):
-                nc.tensor.transpose(bank[:, c, :], bdt[:, P * c : P * (c + 1)], identb[:])
-            turned["bd"] = bank
+        def add_bias(c, j):
+            if j % 2 == 0:
+                made = work.tile([P, 2, O], F32, name="z", bufs=3)
+                zs[c, j // 2] = made
+            nc.vector.tensor_tensor(out=zs[c, j // 2][:, j % 2, :], in0=held["dec", c, j][:], in1=bdt[:], op=ADD)
 
-        def bias_copy():
-            nc.vector.tensor_copy(out=bdc[:].unsqueeze(2), in_=turned["bd"][:, :, 0:1])
-
-        yt = {}
-
-        def decode_t(j):
-            made = outs.tile([P, 4, B], F32, name="yt", bufs=1)
-            yt[j] = made
-            for c in range(4):
-                acc = ps2.tile([P, B], F32, name="bank2")
-                for w in range(2):
-                    a = PARTS[j][w]
-                    nc.tensor.matmul_mx(
-                        out=acc[:],
-                        lhsT=wdw[:, w, 2 * P * c : 2 * P * (c + 1)].bitcast(FP4X4),
-                        lhsT_scale=wds[:, w, P * c : P * (c + 1)],
-                        rhs=qc[a, w][:].bitcast(FP8X4),
-                        rhs_scale=qs[a, w][:],
-                        start=(w == 0),
-                        stop=(w == 1),
-                    )
-                nc.scalar.activation(out=yt[j][:, c, :], in_=acc[:], func=ACT.Sigmoid, bias=bdc[:, c : c + 1])
-
-        ys = {}
-
-        def flip(j, i):
-            bank = ps2.tile([P, O], F32, name="bank2")
-            for c in range(4):
-                nc.tensor.transpose(bank[:, P * c : P * (c + 1)], yt[j][:, c, P * i : P * (i + 1)], ident[:])
-            if i % 2 == 0:
-                made = outs.tile([P, 2, O], F32, name="y")
-                ys[j] = made
-            nc.scalar.copy(out=ys[j][:, i % 2, :], in_=bank[:])
-            if i % 2 == 1:
-                store(ys[j], j, i - 1, 2)
-
-        def store(tile, j, i0, count):
+        def finish(c, j0, count):
+            y = work.tile([P, 2, O], F32, name="y", bufs=6)
+            nc.scalar.activation(out=y[:, 0:count, :], in_=zs[c, j0 // 2][:, j0 % 2 : j0 % 2 + count, :], func=ACT.Sigmoid)
             nc.sync.dma_start(
-                out=out[j, P * i0 : P * (i0 + count), :].rearrange("(i q) o -> q i o", q=P), in_=tile[:, 0:count, :]
+                out=out[j0 : j0 + count, P * c : P * (c + 1), :].rearrange("j q o -> q j o"), in_=y[:, 0:count, :]
             )
 
-        def finish(j, i0, count, slot):
-            y = outs.tile([P, 2, O], F32, name="y")
-            nc.scalar.activation(out=y[:, 0:count, :], in_=zs[j][:, slot : slot + count, :], func=ACT.Sigmoid)
-            store(y, j, i0, count)
-
-        widen(0, 0, 0, "v")
-        widen(0, 0, 1, "v")
-        turn(0, 0)
-        widen(0, 1, 0, "v")
-        widen(0, 1, 1, "v")
-        turn(0, 1)
-        empty(0, 0, "s")
-        empty(0, 1, "s")
-        interleave(0, 0, 2, "v")
-        interleave(0, 2, 4, "s")
-        quant_x(0, 0, 1)
+        spread_scales()
+        widen(0, "v", 0, 1)
+        widen(0, "v", 1, 2)
+        turn(0, 0, 1, ps_dec, "dec")
+        turn(0, 1, 2, ps_dec, "dec")
+        lay_p(0, 0, "v")
+        lay_p(0, 2, "t")
+        halve(bh, braw)
+        widen(1, "s")
+        scale_out(0, 0, "v")
+        scale_out(0, 1, "v")
         quant_p(0, 0, 2)
-        quant_x(0, 1, 2)
+        quant_x(0)
+        empty_p(0, 2)
+        project(0, 0, 0)
+        lay_p(1, 2, "t")
+        turn(1)
+        lay_p(1, 0, "v")
         quant_p(0, 2, 4)
-        for t in range(4):
-            project(0, 0, t, 0, 1)
-        interleave(1, 2, 4, "s")
-        for t in range(4):
-            project(0, 0, t, 1, 2)
-        interleave(1, 0, 2, "v")
-        widen(1, 0, 0, "v")
-        widen(1, 0, 1, "v")
-        gain(0, 0, 0)
+        project(0, 0, 2)
+        squash(0, 0, 0)
+        halve(gh, graw)
+        empty_p(1, 2)
         quant_p(1, 0, 2)
+        scale_out(1, 0, "v")
+        scale_out(1, 1, "v")
+        project(0, 1, 0)
+        squash(0, 0, 2)
         quant_p(1, 2, 4)
-        for t in range(4):
-            project(0, 1, t, 0, 1)
-        turn(1, 0)
-        widen(1, 1, 0, "v")
-        widen(1, 1, 1, "v")
-        turn(1, 1)
-        gain(0, 0, 1)
-        empty(1, 0, "s")
-        empty(1, 1, "s")
-        for t in range(4):
-            project(0, 1, t, 1, 2)
-        gain(0, 1, 0)
-        quant_x(1, 0, 2)
-        quant_q(0, 0, 0, 2)
-        bias_columns()
-        for w in range(2):
-            for t in range(4):
-                project(1, w, t)
-        gain(0, 1, 1)
-        bias_copy()
-        quant_q(0, 1, 0, 1)
-        quant_q(0, 1, 1, 2)
-        gain(1, 0, 0)
-        gain(1, 0, 1)
-        decode_t(0)
-        quant_q(1, 0, 0, 1)
-        quant_q(1, 0, 1, 2)
-        gain(1, 1, 0)
-        decode(2, 0, 0)
-        decode(2, 1, 1)
-        flip(0, 0)
-        flip(0, 1)
-        finish(2, 0, 2, 0)
-        gain(1, 1, 1)
-        quant_q(1, 1, 0, 1)
-        decode(2, 2, 0)
-        quant_q(1, 1, 1, 2)
-        decode(2, 3, 1)
-        flip(0, 2)
-        flip(0, 3)
-        finish(2, 2, 2, 0)
-        for i in (0, 2):
-            for j in (1, 3):
-                decode(j, i, 0)
-                if (i, j) == (2, 3):
-                    finish(j, i, 1, 0)
-                decode(j, i + 1, 1)
-                if (i, j) == (2, 3):
-                    finish(j, i + 1, 1, 1)
-                else:
-                    finish(j, i, 2, 0)
+        quant_x(1)
+        project(0, 1, 2)
+        last = CHUNKS - 1
+        for s in range(CHUNKS + 1):
+            if s < CHUNKS:
+                gain(s, 0)
+                squash(s, 1, 0)
+                squash(s, 1, 2)
+            if 0 < s < last:
+                scale_out(s + 1, 0, "s")
+                scale_out(s + 1, 1, "s")
+            if 0 < s:
+                add_bias(s - 1, 0)
+                add_bias(s - 1, 1)
+            if 0 < s < last:
+                quant_x(s + 1)
+            if s == last:
+                quant_q(s, 0, 1)
+                decode(s, 0, 0, 1)
+                decode(s, 1, 0, 1)
+                decode(s, 2, 0, 1, ps_proj, "proj")
+                decode(s, 3, 0, 1, ps_proj, "proj")
+            if s < last:
+                project(s + 1, 0, 0)
+                project(s + 1, 0, 2)
+            if s < CHUNKS:
+                gain(s, 1)
+            if 1 < s < CHUNKS:
+                finish(s - 2, 2, 2)
+            if s + 2 < CHUNKS:
+                widen(s + 2, "s")
+            if 0 < s < CHUNKS:
+                finish(s - 1, 0, 2)
+            if 0 < s:
+                add_bias(s - 1, 2)
+            if s < last:
+                squash(s + 1, 0, 0)
+                project(s + 1, 1, 0)
+                squash(s + 1, 0, 2)
+                quant_q(s, 0, 2)
+            if s == last:
+                quant_q(s, 1, 2)
+            if s == last:
+                finish(s - 1, 2, 1)
+            if 0 < s:
+                add_bias(s - 1, 3)
+            if s == last:
+                finish(s - 1, 3, 1)
+            if s + 2 < CHUNKS:
+                turn(s + 2)
+            if s < last:
+                project(s + 1, 1, 2)
+                for j in range(4):
+                    decode(s, j)
+            if s == last:
+                for j in range(4):
+                    decode(s, j, 1, 2)
+        for j in range(4):
+            finish(last, j, 1)

@@ -36,7 +36,7 @@ def tile_switchtabmutualsalientswap_d2p_kernel(tc, x_bytes, x_scale, p, b, g, wd
         work = ctx.enter_context(tc.tile_pool(name="work", bufs=2))
         ps_proj = ctx.enter_context(tc.psum_pool(name="ps_proj", bufs=3))
         ps_dec = ctx.enter_context(tc.psum_pool(name="ps_dec", bufs=4))
-        ps_x = ctx.enter_context(tc.psum_pool(name="ps_x", bufs=1))
+        ps_g = ctx.enter_context(tc.psum_pool(name="ps_g", bufs=1))
         ctx.enter_context(tc.manual_schedule())
 
         def kept(shape, dtype, label):
@@ -57,6 +57,8 @@ def tile_switchtabmutualsalientswap_d2p_kernel(tc, x_bytes, x_scale, p, b, g, wd
         make_identity(nc, ident[:])
         identb = kept([P, P], BF16, "identb")
         make_identity(nc, identb[:])
+        halfb = kept([P, P], BF16, "halfb")
+        nc.gpsimd.tensor_scalar(out=halfb[:], in0=identb[:], scalar1=0.5, scalar2=0.0, op0=MULT, op1=ADD)
         blocks = kept([P, P], F32, "blocks")
         nc.vector.memset(blocks[:], 0.0)
         for quad in range(4):
@@ -112,6 +114,11 @@ def tile_switchtabmutualsalientswap_d2p_kernel(tc, x_bytes, x_scale, p, b, g, wd
         def halve(dst, src):
             nc.scalar.activation(out=dst[:], in_=src[:].rearrange("q a t -> q (a t)"), func=ACT.Copy, scale=0.5)
 
+        gp = ps_g.tile([P, 2 * T4], F32, name="gp")
+
+        def gain_to_psum():
+            nc.tensor.matmul(out=gp[:], lhsT=halfb[:], rhs=graw[:].rearrange("q a t -> q (a t)"), start=True, stop=True)
+
         xw = {}
 
         def widen(c, engine, a0=0, a1=V):
@@ -125,7 +132,7 @@ def tile_switchtabmutualsalientswap_d2p_kernel(tc, x_bytes, x_scale, p, b, g, wd
             else:
                 nc.scalar.copy(out=xw[c][:, cols], in_=src)
 
-        def turn(c, a0=0, a1=V, pool=ps_x, label="xt"):
+        def turn(c, a0=0, a1=V, pool=ps_proj, label="proj"):
             bank = pool.tile([P, a1 - a0, 2, P], F32, name=label)
             for a in range(a0, a1):
                 words = xw[c][:, D * a : D * (a + 1)].bitcast(F32)
@@ -221,14 +228,14 @@ def tile_switchtabmutualsalientswap_d2p_kernel(tc, x_bytes, x_scale, p, b, g, wd
 
         qg = {}
 
-        def gain(c, w):
+        def gain(c, w, engine, factor):
             if w == 0:
-                made = work.tile([P, 2, N * T4], BF16, name="qg", align_bytes=64)
+                made = work.tile([P, 2, N * T4], BF16, name="qg", align_bytes=64, bufs=1)
                 qg[c] = made
-            nc.vector.tensor_tensor(
+            engine.tensor_tensor(
                 out=qg[c][:, w, :].rearrange("q (n i t) -> q n t i", i=4, t=T4),
                 in0=th[c, w][:].rearrange("q t (n i) -> q n t i", i=4),
-                in1=gh[:, T4 * w : T4 * (w + 1)].unsqueeze(1).unsqueeze(3).to_broadcast([P, N // 4, T4, 4]),
+                in1=factor[:, T4 * w : T4 * (w + 1)].unsqueeze(1).unsqueeze(3).to_broadcast([P, N // 4, T4, 4]),
                 op=MULT,
             )
 
@@ -269,12 +276,12 @@ def tile_switchtabmutualsalientswap_d2p_kernel(tc, x_bytes, x_scale, p, b, g, wd
 
         def add_bias(c, j):
             if j % 2 == 0:
-                made = work.tile([P, 2, O], F32, name="z", bufs=3)
+                made = work.tile([P, 2, O], F32, name="z", bufs=4)
                 zs[c, j // 2] = made
             nc.vector.tensor_tensor(out=zs[c, j // 2][:, j % 2, :], in0=held["dec", c, j][:], in1=bdt[:], op=ADD)
 
         def finish(c, j0, count):
-            y = work.tile([P, 2, O], F32, name="y", bufs=6)
+            y = work.tile([P, 2, O], F32, name="y", bufs=8)
             nc.scalar.activation(out=y[:, 0:count, :], in_=zs[c, j0 // 2][:, j0 % 2 : j0 % 2 + count, :], func=ACT.Sigmoid)
             nc.sync.dma_start(
                 out=out[j0 : j0 + count, P * c : P * (c + 1), :].rearrange("j q o -> q j o"), in_=y[:, 0:count, :]
@@ -296,75 +303,105 @@ def tile_switchtabmutualsalientswap_d2p_kernel(tc, x_bytes, x_scale, p, b, g, wd
         empty_p(0, 2)
         project(0, 0, 0)
         lay_p(1, 2, "t")
-        turn(1)
+        turn(1, 0, 2, ps_dec, "dec")
         lay_p(1, 0, "v")
         quant_p(0, 2, 4)
         project(0, 0, 2)
         squash(0, 0, 0)
         halve(gh, graw)
         empty_p(1, 2)
+        widen(2, "s")
         quant_p(1, 0, 2)
         scale_out(1, 0, "v")
         scale_out(1, 1, "v")
+        gain_to_psum()
         project(0, 1, 0)
+        turn(2, 0, 2, ps_dec, "dec")
         squash(0, 0, 2)
         quant_p(1, 2, 4)
         quant_x(1)
         project(0, 1, 2)
-        last = CHUNKS - 1
-        for s in range(CHUNKS + 1):
-            if s < CHUNKS:
-                gain(s, 0)
-                squash(s, 1, 0)
-                squash(s, 1, 2)
-            if 0 < s < last:
-                scale_out(s + 1, 0, "s")
-                scale_out(s + 1, 1, "s")
-            if 0 < s:
-                add_bias(s - 1, 0)
-                add_bias(s - 1, 1)
-            if 0 < s < last:
-                quant_x(s + 1)
-            if s == last:
-                quant_q(s, 0, 1)
-                decode(s, 0, 0, 1)
-                decode(s, 1, 0, 1)
-                decode(s, 2, 0, 1, ps_proj, "proj")
-                decode(s, 3, 0, 1, ps_proj, "proj")
-            if s < last:
-                project(s + 1, 0, 0)
-                project(s + 1, 0, 2)
-            if s < CHUNKS:
-                gain(s, 1)
-            if 1 < s < CHUNKS:
-                finish(s - 2, 2, 2)
-            if s + 2 < CHUNKS:
-                widen(s + 2, "s")
-            if 0 < s < CHUNKS:
-                finish(s - 1, 0, 2)
-            if 0 < s:
-                add_bias(s - 1, 2)
-            if s < last:
-                squash(s + 1, 0, 0)
-                project(s + 1, 1, 0)
-                squash(s + 1, 0, 2)
-                quant_q(s, 0, 2)
-            if s == last:
-                quant_q(s, 1, 2)
-            if s == last:
-                finish(s - 1, 2, 1)
-            if 0 < s:
-                add_bias(s - 1, 3)
-            if s == last:
-                finish(s - 1, 3, 1)
-            if s + 2 < CHUNKS:
-                turn(s + 2)
-            if s < last:
-                project(s + 1, 1, 2)
-                for j in range(4):
-                    decode(s, j)
-            if s == last:
-                for j in range(4):
-                    decode(s, j, 1, 2)
+        gain(0, 0, nc.vector, gp)
+        squash(0, 1, 0)
+        project(1, 0, 0)
+        squash(0, 1, 2)
+        project(1, 0, 2)
+        scale_out(2, 0, "v")
+        scale_out(2, 1, "v")
+        gain(0, 1, nc.vector, gp)
+        squash(1, 0, 0)
+        project(1, 1, 0)
+        squash(1, 0, 2)
+        project(1, 1, 2)
+        widen(3, "s")
+        turn(3, 0, 2, ps_dec, "dec")
+        quant_x(2)
+        quant_q(0, 0, 2)
+        gain(1, 0, nc.gpsimd, gh)
+        squash(1, 1, 0)
+        project(2, 0, 0)
+        decode(0, 0)
+        squash(1, 1, 2)
+        project(2, 0, 2)
+        decode(0, 1)
+        scale_out(3, 0, "v")
+        scale_out(3, 1, "v")
+        gain(1, 1, nc.vector, gp)
+        squash(2, 0, 0)
+        project(2, 1, 0)
+        decode(0, 2)
+        squash(2, 0, 2)
+        project(2, 1, 2)
+        decode(0, 3)
+        add_bias(0, 0)
+        add_bias(0, 1)
+        quant_x(3)
+        quant_q(1, 0, 2)
+        gain(2, 0, nc.gpsimd, gh)
+        squash(2, 1, 0)
+        squash(2, 1, 2)
+        decode(1, 0)
+        project(3, 0, 0)
+        decode(1, 1)
+        project(3, 0, 2)
+        project(3, 1, 0)
+        add_bias(0, 2)
+        add_bias(0, 3)
+        decode(1, 2)
+        decode(1, 3)
+        finish(0, 0, 2)
+        gain(2, 1, nc.vector, gp)
+        squash(3, 0, 0)
+        project(3, 1, 2)
+        squash(3, 0, 2)
+        finish(0, 2, 2)
+        add_bias(1, 0)
+        add_bias(1, 1)
+        quant_q(2, 0, 2)
+        gain(3, 0, nc.gpsimd, gh)
+        decode(2, 0)
+        decode(2, 1)
+        add_bias(1, 2)
+        add_bias(1, 3)
+        decode(2, 2)
+        decode(2, 3)
+        squash(3, 1, 0)
+        squash(3, 1, 2)
+        finish(1, 0, 2)
+        finish(1, 2, 2)
+        add_bias(2, 0)
+        gain(3, 1, nc.vector, gp)
+        add_bias(2, 1)
+        quant_q(3, 0, 2)
+        decode(3, 0)
+        decode(3, 1)
+        add_bias(2, 2)
+        add_bias(2, 3)
+        decode(3, 2)
+        decode(3, 3)
+        finish(2, 0, 2)
+        finish(2, 2, 1)
+        finish(2, 3, 1)
         for j in range(4):
-            finish(last, j, 1)
+            add_bias(3, j)
+            finish(3, j, 1)

@@ -43,7 +43,7 @@ def tile_switchtabmutualsalientswap_d2p_kernel(tc, x_bytes, x_scale, p, b, g, wd
             made = keep.tile(shape, dtype, name=label, align_bytes=64)
             return made
 
-        xs_rows = kept([P, V * CHUNKS], F32, "xs_rows")
+        xs_rows = kept([P, V * CHUNKS * 5], F32, "xs_rows")
         nc.vector.memset(xs_rows[:], 0.0)
         braw = kept([P, V, T4], BF16, "braw")
         graw = kept([P, 2, T4], BF16, "graw")
@@ -83,7 +83,8 @@ def tile_switchtabmutualsalientswap_d2p_kernel(tc, x_bytes, x_scale, p, b, g, wd
 
         load_x(0)
         with nc.allow_non_contiguous_dma(reason="32 scales, turned on the way in"):
-            nc.sync.dma_start(out=xs_rows[0:P:32, :], in_=x_scale.rearrange("a i j -> j (a i)"))
+            nc.sync.dma_start(out=xs_rows[0:P:32, 0:8], in_=x_scale.rearrange("a i j -> j (a i)"))
+        nc.sync.dma_start(out=xs_rows[0:P:32, 8:40], in_=x_scale.rearrange("a i j -> (a i j)").partition_broadcast(4))
         load_p(0)
         nc.sync.dma_start(out=braw[:], in_=b.rearrange("a (q t) -> q a t", t=T4))
         load_x(1)
@@ -101,13 +102,13 @@ def tile_switchtabmutualsalientswap_d2p_kernel(tc, x_bytes, x_scale, p, b, g, wd
         bdt = kept([P, O], BF16, "bdt")
         nc.sync.dma_start(out=bdt[:], in_=bd.partition_broadcast(P))
 
-        xs = kept([P, V * CHUNKS], F32, "xs")
+        xs = kept([P, V * CHUNKS * 5], F32, "xs")
         bh = kept([P, V * T4], F32, "bh")
         gh = kept([P, 2 * T4], F32, "gh")
         held = {}
 
         def spread_scales():
-            bank = ps_dec.tile([P, V * CHUNKS], F32, name="dec")
+            bank = ps_dec.tile([P, V * CHUNKS * 5], F32, name="dec")
             nc.tensor.matmul(out=bank[:], lhsT=blocks[:], rhs=xs_rows[:], start=True, stop=True)
             nc.scalar.copy(out=xs[:], in_=bank[:])
 
@@ -120,10 +121,11 @@ def tile_switchtabmutualsalientswap_d2p_kernel(tc, x_bytes, x_scale, p, b, g, wd
             nc.tensor.matmul(out=gp[:], lhsT=halfb[:], rhs=graw[:].rearrange("q a t -> q (a t)"), start=True, stop=True)
 
         xw = {}
+        xg = {}
 
         def widen(c, engine, a0=0, a1=V):
             if a0 == 0:
-                made = work.tile([P, V * D], BF16, name="xw", align_bytes=64)
+                made = work.tile([P, V * D], BF16, name="xw", align_bytes=64, bufs=4)
                 xw[c] = made
             cols = slice(D * a0, D * a1)
             src = xb[c][:].rearrange("q a k -> q (a k)")[:, cols].bitcast(FP8)
@@ -132,6 +134,29 @@ def tile_switchtabmutualsalientswap_d2p_kernel(tc, x_bytes, x_scale, p, b, g, wd
             else:
                 nc.scalar.copy(out=xw[c][:, cols], in_=src)
 
+        def widen_scaled(c, a, engine):
+            if c not in xw:
+                made = work.tile([P, V * D], BF16, name="xw", align_bytes=64, bufs=4)
+                xw[c] = made
+            for j in range(4):
+                cols = slice(D * a + P * j, D * a + P * (j + 1))
+                at = 8 + 16 * a + 4 * c + j
+                src = xb[c][:].rearrange("q a k -> q (a k)")[:, cols].bitcast(FP8)
+                if engine == "v":
+                    nc.vector.tensor_scalar(out=xw[c][:, cols], in0=src, scalar1=xs[:, at : at + 1], scalar2=None, op0=MULT)
+                else:
+                    nc.scalar.activation(out=xw[c][:, cols], in_=src, func=ACT.Copy, scale=xs[:, at : at + 1])
+
+        def copy_x(c, engine):
+            made = work.tile([P, V, P * T4], BF16, name="xg", align_bytes=64, bufs=4)
+            xg[c] = made
+            dst = made[:].bitcast(F32).rearrange("q a (r u) -> q a r u", u=2)
+            src = held["xtb", c][:].rearrange("q a u r -> q a r u")
+            if engine == "v":
+                nc.vector.tensor_copy(out=dst, in_=src)
+            else:
+                nc.scalar.copy(out=dst, in_=src)
+
         def turn(c, a0=0, a1=V, pool=ps_proj, label="proj"):
             bank = pool.tile([P, a1 - a0, 2, P], F32, name=label)
             for a in range(a0, a1):
@@ -139,12 +164,11 @@ def tile_switchtabmutualsalientswap_d2p_kernel(tc, x_bytes, x_scale, p, b, g, wd
                 for u in range(2):
                     nc.tensor.transpose(bank[:, a - a0, u, :], words[:, u : D // 2 : 2], ident[:])
                 held["xt", c, a] = bank[:, a - a0, :, :]
-
-        xg = {}
+            held["xtb", c] = bank
 
         def scale_out(c, a, engine):
             if c not in xg:
-                made = work.tile([P, V, P * T4], BF16, name="xg", align_bytes=64)
+                made = work.tile([P, V, P * T4], BF16, name="xg", align_bytes=64, bufs=4)
                 xg[c] = made
             src = held["xt", c, a].bitcast(BF16).rearrange("q u (r e) -> q r u e", e=2)
             dst = xg[c][:, a, :].rearrange("q (r u e) -> q r u e", u=2, e=2)
@@ -295,7 +319,8 @@ def tile_switchtabmutualsalientswap_d2p_kernel(tc, x_bytes, x_scale, p, b, g, wd
         lay_p(0, 0, "v")
         lay_p(0, 2, "t")
         halve(bh, braw)
-        widen(1, "s")
+        widen_scaled(1, 0, "s")
+        widen_scaled(1, 1, "s")
         scale_out(0, 0, "v")
         scale_out(0, 1, "v")
         quant_p(0, 0, 2)
@@ -310,48 +335,47 @@ def tile_switchtabmutualsalientswap_d2p_kernel(tc, x_bytes, x_scale, p, b, g, wd
         squash(0, 0, 0)
         halve(gh, graw)
         empty_p(1, 2)
-        widen(2, "s")
+        widen_scaled(2, 0, "v")
+        widen_scaled(2, 1, "v")
         quant_p(1, 0, 2)
-        scale_out(1, 0, "v")
-        scale_out(1, 1, "v")
+        copy_x(1, "s")
         gain_to_psum()
         project(0, 1, 0)
         turn(2, 0, 2, ps_dec, "dec")
         squash(0, 0, 2)
+        widen_scaled(3, 0, "v")
         quant_p(1, 2, 4)
         quant_x(1)
+        widen_scaled(3, 1, "v")
         project(0, 1, 2)
         gain(0, 0, nc.vector, gp)
         squash(0, 1, 0)
         project(1, 0, 0)
+        turn(3, 0, 2, ps_dec, "dec")
         squash(0, 1, 2)
         project(1, 0, 2)
-        scale_out(2, 0, "v")
-        scale_out(2, 1, "v")
+        copy_x(2, "s")
         gain(0, 1, nc.vector, gp)
         squash(1, 0, 0)
         project(1, 1, 0)
         squash(1, 0, 2)
         project(1, 1, 2)
-        widen(3, "s")
-        turn(3, 0, 2, ps_dec, "dec")
         quant_x(2)
         quant_q(0, 0, 2)
         gain(1, 0, nc.gpsimd, gh)
         squash(1, 1, 0)
         project(2, 0, 0)
-        decode(0, 0)
         squash(1, 1, 2)
         project(2, 0, 2)
+        decode(0, 0)
         decode(0, 1)
-        scale_out(3, 0, "v")
-        scale_out(3, 1, "v")
+        copy_x(3, "v")
         gain(1, 1, nc.vector, gp)
         squash(2, 0, 0)
         project(2, 1, 0)
-        decode(0, 2)
         squash(2, 0, 2)
         project(2, 1, 2)
+        decode(0, 2)
         decode(0, 3)
         add_bias(0, 0)
         add_bias(0, 1)
@@ -360,10 +384,10 @@ def tile_switchtabmutualsalientswap_d2p_kernel(tc, x_bytes, x_scale, p, b, g, wd
         gain(2, 0, nc.gpsimd, gh)
         squash(2, 1, 0)
         squash(2, 1, 2)
-        decode(1, 0)
         project(3, 0, 0)
-        decode(1, 1)
         project(3, 0, 2)
+        decode(1, 0)
+        decode(1, 1)
         project(3, 1, 0)
         add_bias(0, 2)
         add_bias(0, 3)
@@ -390,16 +414,17 @@ def tile_switchtabmutualsalientswap_d2p_kernel(tc, x_bytes, x_scale, p, b, g, wd
         finish(1, 0, 2)
         finish(1, 2, 2)
         add_bias(2, 0)
-        gain(3, 1, nc.vector, gp)
         add_bias(2, 1)
-        quant_q(3, 0, 2)
+        gain(3, 1, nc.vector, gp)
+        finish(2, 0, 2)
+        quant_q(3, 0, 1)
+        quant_q(3, 1, 2)
         decode(3, 0)
         decode(3, 1)
         add_bias(2, 2)
         add_bias(2, 3)
         decode(3, 2)
         decode(3, 3)
-        finish(2, 0, 2)
         finish(2, 2, 1)
         finish(2, 3, 1)
         for j in range(4):

@@ -35,7 +35,7 @@ def tile_switchtabmutualsalientswap_d2p_kernel(tc, x_bytes, x_scale, p, b, g, wd
         keep = ctx.enter_context(tc.tile_pool(name="keep", bufs=1))
         work = ctx.enter_context(tc.tile_pool(name="work", bufs=2))
         ps_proj = ctx.enter_context(tc.psum_pool(name="ps_proj", bufs=3))
-        ps_dec = ctx.enter_context(tc.psum_pool(name="ps_dec", bufs=4))
+        ps_dec = ctx.enter_context(tc.psum_pool(name="ps_dec", bufs=1))
         ps_g = ctx.enter_context(tc.psum_pool(name="ps_g", bufs=1))
         ctx.enter_context(tc.manual_schedule())
 
@@ -108,7 +108,7 @@ def tile_switchtabmutualsalientswap_d2p_kernel(tc, x_bytes, x_scale, p, b, g, wd
         held = {}
 
         def spread_scales():
-            bank = ps_dec.tile([P, V * CHUNKS * 5], F32, name="dec")
+            bank = ps_dec.tile([P, V * CHUNKS * 5], F32, name="dec0")
             nc.tensor.matmul(out=bank[:], lhsT=blocks[:], rhs=xs_rows[:], start=True, stop=True)
             nc.scalar.copy(out=xs[:], in_=bank[:])
 
@@ -198,15 +198,17 @@ def tile_switchtabmutualsalientswap_d2p_kernel(tc, x_bytes, x_scale, p, b, g, wd
             pc[w] = kept([P, H], U32, "pc%d" % w)
             psc[w] = kept([P, H], U8, "psc%d" % w)
 
-        def lay_p(w, t0, engine, count=2):
+        def lay_p(w, t0, engine, label="", count=2):
             dst = pg[w][:].rearrange("q (t m j) -> q t m j", t=T4, j=T4)[:, t0 : t0 + count]
             src = praw[w][:].rearrange("q j (m t) -> q t m j", t=T4)[:, t0 : t0 + count]
             if engine == "v":
-                nc.vector.tensor_copy(out=dst, in_=src)
+                nc.vector.tensor_copy(
+                    out=dst.rearrange("q t (m i) j -> q m t i j", i=2), in_=src.rearrange("q t (m i) j -> q m t i j", i=2)
+                )
             elif engine == "s":
                 nc.scalar.copy(out=dst, in_=src)
             else:
-                bank = ps_dec.tile([P, 2, P * T4], BF16, name="dec")
+                bank = ps_dec.tile([P, 2, P * T4], BF16, name=label)
                 for t in range(2):
                     nc.tensor.matmul(out=bank[:, t, :], lhsT=identb[:], rhs=src[:, t], start=True, stop=True)
                 held["pt", w, t0] = bank
@@ -252,14 +254,14 @@ def tile_switchtabmutualsalientswap_d2p_kernel(tc, x_bytes, x_scale, p, b, g, wd
 
         qg = {}
 
-        def gain(c, w, engine, factor):
-            if w == 0:
+        def gain(c, w, engine, factor, n0=0, n1=N):
+            if c not in qg:
                 made = work.tile([P, 2, N * T4], BF16, name="qg", align_bytes=64, bufs=1)
                 qg[c] = made
             engine.tensor_tensor(
-                out=qg[c][:, w, :].rearrange("q (n i t) -> q n t i", i=4, t=T4),
-                in0=th[c, w][:].rearrange("q t (n i) -> q n t i", i=4),
-                in1=factor[:, T4 * w : T4 * (w + 1)].unsqueeze(1).unsqueeze(3).to_broadcast([P, N // 4, T4, 4]),
+                out=qg[c][:, w, T4 * n0 : T4 * n1].rearrange("q (n i t) -> q n t i", i=2, t=T4),
+                in0=th[c, w][:, :, n0:n1].rearrange("q t (n i) -> q n t i", i=2),
+                in1=factor[:, T4 * w : T4 * (w + 1)].unsqueeze(1).unsqueeze(3).to_broadcast([P, (n1 - n0) // 2, T4, 2]),
                 op=MULT,
             )
 
@@ -279,7 +281,7 @@ def tile_switchtabmutualsalientswap_d2p_kernel(tc, x_bytes, x_scale, p, b, g, wd
                 in_=qg[c][:, w0:w1, :].rearrange("q w n -> q (w n)"),
             )
 
-        def decode(c, j, w0=0, w1=2, pool=ps_dec, label="dec"):
+        def decode(c, j, label, pool=ps_dec, w0=0, w1=2):
             if w0 == 0:
                 made = pool.tile([P, O], F32, name=label)
                 held["dec", c, j] = made
@@ -314,21 +316,21 @@ def tile_switchtabmutualsalientswap_d2p_kernel(tc, x_bytes, x_scale, p, b, g, wd
         spread_scales()
         widen(0, "v", 0, 1)
         widen(0, "v", 1, 2)
-        turn(0, 0, 1, ps_dec, "dec")
-        turn(0, 1, 2, ps_dec, "dec")
+        turn(0, 0, 1, ps_dec, "dec1")
+        turn(0, 1, 2, ps_dec, "dec2")
         lay_p(0, 0, "v")
-        lay_p(0, 2, "t")
+        lay_p(0, 2, "t", "dec3")
+        scale_out(0, 0, "s")
+        scale_out(0, 1, "s")
         halve(bh, braw)
         widen_scaled(1, 0, "s")
-        widen_scaled(1, 1, "s")
-        scale_out(0, 0, "v")
-        scale_out(0, 1, "v")
         quant_p(0, 0, 2)
         quant_x(0)
+        widen_scaled(1, 1, "v")
         empty_p(0, 2)
         project(0, 0, 0)
-        lay_p(1, 2, "t")
-        turn(1, 0, 2, ps_dec, "dec")
+        lay_p(1, 2, "t", "dec0")
+        turn(1, 0, 2, ps_dec, "dec1")
         lay_p(1, 0, "v")
         quant_p(0, 2, 4)
         project(0, 0, 2)
@@ -341,7 +343,7 @@ def tile_switchtabmutualsalientswap_d2p_kernel(tc, x_bytes, x_scale, p, b, g, wd
         copy_x(1, "s")
         gain_to_psum()
         project(0, 1, 0)
-        turn(2, 0, 2, ps_dec, "dec")
+        turn(2, 0, 2, ps_dec, "dec2")
         squash(0, 0, 2)
         widen_scaled(3, 0, "v")
         quant_p(1, 2, 4)
@@ -351,7 +353,7 @@ def tile_switchtabmutualsalientswap_d2p_kernel(tc, x_bytes, x_scale, p, b, g, wd
         gain(0, 0, nc.vector, gp)
         squash(0, 1, 0)
         project(1, 0, 0)
-        turn(3, 0, 2, ps_dec, "dec")
+        turn(3, 0, 2, ps_dec, "dec3")
         squash(0, 1, 2)
         project(1, 0, 2)
         copy_x(2, "s")
@@ -362,38 +364,40 @@ def tile_switchtabmutualsalientswap_d2p_kernel(tc, x_bytes, x_scale, p, b, g, wd
         project(1, 1, 2)
         quant_x(2)
         quant_q(0, 0, 2)
-        gain(1, 0, nc.gpsimd, gh)
+        gain(1, 0, nc.gpsimd, gh, 0, 224)
         squash(1, 1, 0)
         project(2, 0, 0)
         squash(1, 1, 2)
         project(2, 0, 2)
-        decode(0, 0)
-        decode(0, 1)
+        decode(0, 0, "dec0")
+        decode(0, 1, "dec1")
         copy_x(3, "v")
+        gain(1, 0, nc.vector, gp, 224, N)
         gain(1, 1, nc.vector, gp)
         squash(2, 0, 0)
         project(2, 1, 0)
+        decode(0, 2, "dec2")
         squash(2, 0, 2)
         project(2, 1, 2)
-        decode(0, 2)
-        decode(0, 3)
+        decode(0, 3, "dec3")
         add_bias(0, 0)
         add_bias(0, 1)
         quant_x(3)
         quant_q(1, 0, 2)
-        gain(2, 0, nc.gpsimd, gh)
+        gain(2, 0, nc.gpsimd, gh, 0, 224)
         squash(2, 1, 0)
         squash(2, 1, 2)
         project(3, 0, 0)
         project(3, 0, 2)
-        decode(1, 0)
-        decode(1, 1)
+        decode(1, 0, "dec0")
+        decode(1, 1, "dec1")
         project(3, 1, 0)
         add_bias(0, 2)
         add_bias(0, 3)
-        decode(1, 2)
-        decode(1, 3)
+        decode(1, 2, "dec2")
+        decode(1, 3, "dec3")
         finish(0, 0, 2)
+        gain(2, 0, nc.vector, gp, 224, N)
         gain(2, 1, nc.vector, gp)
         squash(3, 0, 0)
         project(3, 1, 2)
@@ -402,29 +406,30 @@ def tile_switchtabmutualsalientswap_d2p_kernel(tc, x_bytes, x_scale, p, b, g, wd
         add_bias(1, 0)
         add_bias(1, 1)
         quant_q(2, 0, 2)
-        gain(3, 0, nc.gpsimd, gh)
-        decode(2, 0)
-        decode(2, 1)
+        gain(3, 0, nc.gpsimd, gh, 0, 224)
+        decode(2, 0, "dec0")
+        decode(2, 1, "dec1")
         add_bias(1, 2)
         add_bias(1, 3)
-        decode(2, 2)
-        decode(2, 3)
         squash(3, 1, 0)
         squash(3, 1, 2)
         finish(1, 0, 2)
         finish(1, 2, 2)
         add_bias(2, 0)
         add_bias(2, 1)
+        decode(2, 2, "dec0")
+        decode(2, 3, "dec1")
+        gain(3, 0, nc.vector, gp, 224, N)
         gain(3, 1, nc.vector, gp)
         finish(2, 0, 2)
         quant_q(3, 0, 1)
         quant_q(3, 1, 2)
-        decode(3, 0)
-        decode(3, 1)
+        decode(3, 0, "dec2")
+        decode(3, 1, "dec3")
+        decode(3, 2, "proj", ps_proj)
+        decode(3, 3, "proj", ps_proj)
         add_bias(2, 2)
         add_bias(2, 3)
-        decode(3, 2)
-        decode(3, 3)
         finish(2, 2, 1)
         finish(2, 3, 1)
         for j in range(4):

@@ -54,11 +54,8 @@ def tile_switchtabmutualsalientswap_d2p_kernel(tc, x_bytes, x_scale, p, b, g, wd
         nc.scalar.activation(out=warmed[:], in_=warm[:], func=ACT.Sigmoid)
 
         ident = kept([P, P], F32, "ident")
-        make_identity(nc, ident[:])
-        identb = kept([P, P], BF16, "identb")
-        make_identity(nc, identb[:])
-        halfb = kept([P, P], BF16, "halfb")
-        nc.gpsimd.tensor_scalar(out=halfb[:], in0=identb[:], scalar1=0.5, scalar2=0.0, op0=MULT, op1=ADD)
+        nc.vector.memset(ident[:], 0.0)
+        make_identity(nc, ident[:], nomemset=True)
         blocks = kept([P, P], F32, "blocks")
         nc.vector.memset(blocks[:], 0.0)
         for quad in range(4):
@@ -66,6 +63,11 @@ def tile_switchtabmutualsalientswap_d2p_kernel(tc, x_bytes, x_scale, p, b, g, wd
             nc.vector.memset(blocks[rows, rows], 1.0)
         wds = kept([P, 2, O], U8, "wds")
         nc.vector.memset(wds[:].rearrange("q g n -> q (g n)").bitcast(I32), 0)
+
+        identb = kept([P, P], BF16, "identb")
+        nc.vector.tensor_copy(out=identb[:], in_=ident[:])
+        halfb = kept([P, P], BF16, "halfb")
+        nc.vector.tensor_scalar(out=halfb[:], in0=ident[:], scalar1=0.5, scalar2=None, op0=MULT)
 
         xb = {}
 
@@ -259,9 +261,9 @@ def tile_switchtabmutualsalientswap_d2p_kernel(tc, x_bytes, x_scale, p, b, g, wd
                 made = work.tile([P, 2, N * T4], BF16, name="qg", align_bytes=64, bufs=1)
                 qg[c] = made
             engine.tensor_tensor(
-                out=qg[c][:, w, T4 * n0 : T4 * n1].rearrange("q (n i t) -> q n t i", i=2, t=T4),
-                in0=th[c, w][:, :, n0:n1].rearrange("q t (n i) -> q n t i", i=2),
-                in1=factor[:, T4 * w : T4 * (w + 1)].unsqueeze(1).unsqueeze(3).to_broadcast([P, (n1 - n0) // 2, T4, 2]),
+                out=qg[c][:, w, T4 * n0 : T4 * n1].rearrange("q (n i t) -> q n t i", i=4, t=T4),
+                in0=th[c, w][:, :, n0:n1].rearrange("q t (n i) -> q n t i", i=4),
+                in1=factor[:, T4 * w : T4 * (w + 1)].unsqueeze(1).unsqueeze(3).to_broadcast([P, (n1 - n0) // 4, T4, 4]),
                 op=MULT,
             )
 
@@ -340,16 +342,16 @@ def tile_switchtabmutualsalientswap_d2p_kernel(tc, x_bytes, x_scale, p, b, g, wd
         widen_scaled(2, 0, "v")
         widen_scaled(2, 1, "v")
         quant_p(1, 0, 2)
+        quant_p(1, 2, 4)
         copy_x(1, "s")
         gain_to_psum()
         project(0, 1, 0)
-        turn(2, 0, 2, ps_dec, "dec2")
         squash(0, 0, 2)
+        project(0, 1, 2)
+        turn(2, 0, 2, ps_dec, "dec2")
         widen_scaled(3, 0, "v")
-        quant_p(1, 2, 4)
         quant_x(1)
         widen_scaled(3, 1, "v")
-        project(0, 1, 2)
         gain(0, 0, nc.vector, gp)
         squash(0, 1, 0)
         project(1, 0, 0)

@@ -204,9 +204,7 @@ def tile_switchtabmutualsalientswap_d2p_kernel(tc, x_bytes, x_scale, p, b, g, wd
             dst = pg[w][:].rearrange("q (t m j) -> q t m j", t=T4, j=T4)[:, t0 : t0 + count]
             src = praw[w][:].rearrange("q j (m t) -> q t m j", t=T4)[:, t0 : t0 + count]
             if engine == "v":
-                nc.vector.tensor_copy(
-                    out=dst.rearrange("q t (m i) j -> q m t i j", i=2), in_=src.rearrange("q t (m i) j -> q m t i j", i=2)
-                )
+                nc.vector.tensor_copy(out=dst, in_=src)
             elif engine == "s":
                 nc.scalar.copy(out=dst, in_=src)
             else:
@@ -261,9 +259,9 @@ def tile_switchtabmutualsalientswap_d2p_kernel(tc, x_bytes, x_scale, p, b, g, wd
                 made = work.tile([P, 2, N * T4], BF16, name="qg", align_bytes=64, bufs=1)
                 qg[c] = made
             engine.tensor_tensor(
-                out=qg[c][:, w, T4 * n0 : T4 * n1].rearrange("q (n i t) -> q n t i", i=4, t=T4),
-                in0=th[c, w][:, :, n0:n1].rearrange("q t (n i) -> q n t i", i=4),
-                in1=factor[:, T4 * w : T4 * (w + 1)].unsqueeze(1).unsqueeze(3).to_broadcast([P, (n1 - n0) // 4, T4, 4]),
+                out=qg[c][:, w, T4 * n0 : T4 * n1].rearrange("q (n i t) -> q n t i", i=2, t=T4),
+                in0=th[c, w][:, :, n0:n1].rearrange("q t (n i) -> q n t i", i=2),
+                in1=factor[:, T4 * w : T4 * (w + 1)].unsqueeze(1).unsqueeze(3).to_broadcast([P, (n1 - n0) // 2, T4, 2]),
                 op=MULT,
             )
 
@@ -366,7 +364,7 @@ def tile_switchtabmutualsalientswap_d2p_kernel(tc, x_bytes, x_scale, p, b, g, wd
         project(1, 1, 2)
         quant_x(2)
         quant_q(0, 0, 2)
-        gain(1, 0, nc.gpsimd, gh, 0, 224)
+        gain(1, 0, nc.gpsimd, gh)
         squash(1, 1, 0)
         project(2, 0, 0)
         squash(1, 1, 2)
@@ -374,7 +372,6 @@ def tile_switchtabmutualsalientswap_d2p_kernel(tc, x_bytes, x_scale, p, b, g, wd
         decode(0, 0, "dec0")
         decode(0, 1, "dec1")
         copy_x(3, "v")
-        gain(1, 0, nc.vector, gp, 224, N)
         gain(1, 1, nc.vector, gp)
         squash(2, 0, 0)
         project(2, 1, 0)
@@ -386,7 +383,7 @@ def tile_switchtabmutualsalientswap_d2p_kernel(tc, x_bytes, x_scale, p, b, g, wd
         add_bias(0, 1)
         quant_x(3)
         quant_q(1, 0, 2)
-        gain(2, 0, nc.gpsimd, gh, 0, 224)
+        gain(2, 0, nc.gpsimd, gh)
         squash(2, 1, 0)
         squash(2, 1, 2)
         project(3, 0, 0)
@@ -399,7 +396,6 @@ def tile_switchtabmutualsalientswap_d2p_kernel(tc, x_bytes, x_scale, p, b, g, wd
         decode(1, 2, "dec2")
         decode(1, 3, "dec3")
         finish(0, 0, 2)
-        gain(2, 0, nc.vector, gp, 224, N)
         gain(2, 1, nc.vector, gp)
         squash(3, 0, 0)
         project(3, 1, 2)
@@ -408,7 +404,7 @@ def tile_switchtabmutualsalientswap_d2p_kernel(tc, x_bytes, x_scale, p, b, g, wd
         add_bias(1, 0)
         add_bias(1, 1)
         quant_q(2, 0, 2)
-        gain(3, 0, nc.gpsimd, gh, 0, 224)
+        gain(3, 0, nc.gpsimd, gh)
         decode(2, 0, "dec0")
         decode(2, 1, "dec1")
         add_bias(1, 2)
@@ -421,7 +417,6 @@ def tile_switchtabmutualsalientswap_d2p_kernel(tc, x_bytes, x_scale, p, b, g, wd
         add_bias(2, 1)
         decode(2, 2, "dec0")
         decode(2, 3, "dec1")
-        gain(3, 0, nc.vector, gp, 224, N)
         gain(3, 1, nc.vector, gp)
         finish(2, 0, 2)
         quant_q(3, 0, 1)

@@ -43,10 +43,10 @@ def tile_switchtabmutualsalientswap_d2p_kernel(tc, x_bytes, x_scale, p, b, g, wd
             made = keep.tile(shape, dtype, name=label, align_bytes=64)
             return made
 
-        xs_rows = kept([P, V * CHUNKS * 5], F32, "xs_rows")
+        xs_rows = kept([P, V * 16 + V], F32, "xs_rows")
         nc.vector.memset(xs_rows[:], 0.0)
-        braw = kept([P, V, T4], BF16, "braw")
-        graw = kept([P, 2, T4], BF16, "graw")
+        bg_rows = kept([P, H], BF16, "bg_rows")
+        nc.vector.memset(bg_rows[:], 0.0)
 
         warm = kept([P, 1], F32, "warm")
         nc.vector.memset(warm[:], 0.0)
@@ -85,13 +85,13 @@ def tile_switchtabmutualsalientswap_d2p_kernel(tc, x_bytes, x_scale, p, b, g, wd
 
         load_x(0)
         with nc.allow_non_contiguous_dma(reason="32 scales, turned on the way in"):
-            nc.sync.dma_start(out=xs_rows[0:P:32, 0:8], in_=x_scale.rearrange("a i j -> j (a i)"))
-        nc.sync.dma_start(out=xs_rows[0:P:32, 8:40], in_=x_scale.rearrange("a i j -> (a i j)").partition_broadcast(4))
+            nc.sync.dma_start(out=xs_rows[0:P:32, V * 16 : V * 16 + V], in_=x_scale[:, 0, :].rearrange("a j -> j a"))
+        nc.sync.dma_start(out=xs_rows[0:P:32, 0 : V * 16], in_=x_scale.rearrange("a i j -> (a i j)").partition_broadcast(4))
         load_p(0)
-        nc.sync.dma_start(out=braw[:], in_=b.rearrange("a (q t) -> q a t", t=T4))
+        nc.sync.dma_start(out=bg_rows[0:2, :], in_=b)
+        nc.sync.dma_start(out=bg_rows[2:4, :], in_=g.rearrange("(w c) -> w c", w=2))
         load_x(1)
         load_p(1)
-        nc.sync.dma_start(out=graw[:], in_=g.rearrange("(a q t) -> q a t", a=2, t=T4))
         load_x(2)
         load_x(3)
         wdw = kept([P, 2, 2 * O], U8, "wdw")
@@ -104,23 +104,24 @@ def tile_switchtabmutualsalientswap_d2p_kernel(tc, x_bytes, x_scale, p, b, g, wd
         bdt = kept([P, O], BF16, "bdt")
         nc.sync.dma_start(out=bdt[:], in_=bd.partition_broadcast(P))
 
-        xs = kept([P, V * CHUNKS * 5], F32, "xs")
-        bh = kept([P, V * T4], F32, "bh")
-        gh = kept([P, 2 * T4], F32, "gh")
+        xs = kept([P, V + V * 16], F32, "xs")
+        halves = kept([P, T4, 4], F32, "halves")
         held = {}
 
         def spread_scales():
-            bank = ps_dec.tile([P, V * CHUNKS * 5], F32, name="dec0")
+            bank = ps_dec.tile([P, V + V * 16], F32, name="dec0")
             nc.tensor.matmul(out=bank[:], lhsT=blocks[:], rhs=xs_rows[:], start=True, stop=True)
             nc.scalar.copy(out=xs[:], in_=bank[:])
 
-        def halve(dst, src):
-            nc.scalar.activation(out=dst[:], in_=src[:].rearrange("q a t -> q (a t)"), func=ACT.Copy, scale=0.5)
+        gp = ps_g.tile([P, T4, 4], F32, name="gp")
+        gh = halves
 
-        gp = ps_g.tile([P, 2 * T4], F32, name="gp")
+        def turn_rows():
+            for t in range(T4):
+                nc.tensor.matmul(out=gp[:, t, :], lhsT=bg_rows[:, t:H:T4], rhs=halfb[:, 0:4], start=True, stop=True)
 
-        def gain_to_psum():
-            nc.tensor.matmul(out=gp[:], lhsT=halfb[:], rhs=graw[:].rearrange("q a t -> q (a t)"), start=True, stop=True)
+        def copy_rows():
+            nc.scalar.copy(out=halves[:], in_=gp[:])
 
         xw = {}
         xg = {}
@@ -142,7 +143,7 @@ def tile_switchtabmutualsalientswap_d2p_kernel(tc, x_bytes, x_scale, p, b, g, wd
                 xw[c] = made
             for j in range(4):
                 cols = slice(D * a + P * j, D * a + P * (j + 1))
-                at = 8 + 16 * a + 4 * c + j
+                at = 16 * a + 4 * c + j
                 src = xb[c][:].rearrange("q a k -> q (a k)")[:, cols].bitcast(FP8)
                 if engine == "v":
                     nc.vector.tensor_scalar(out=xw[c][:, cols], in0=src, scalar1=xs[:, at : at + 1], scalar2=None, op0=MULT)
@@ -174,7 +175,7 @@ def tile_switchtabmutualsalientswap_d2p_kernel(tc, x_bytes, x_scale, p, b, g, wd
                 xg[c] = made
             src = held["xt", c, a].bitcast(BF16).rearrange("q u (r e) -> q r u e", e=2)
             dst = xg[c][:, a, :].rearrange("q (r u e) -> q r u e", u=2, e=2)
-            at = CHUNKS * a + c
+            at = V * 16 + a
             if engine == "v":
                 nc.vector.tensor_scalar(out=dst, in0=src, scalar1=xs[:, at : at + 1], scalar2=None, op0=MULT)
             else:
@@ -247,9 +248,8 @@ def tile_switchtabmutualsalientswap_d2p_kernel(tc, x_bytes, x_scale, p, b, g, wd
                 th[c, w] = made
             acc = held["proj", c, w, t0]
             for t in range(t0, t0 + 2):
-                at = T4 * w + t
                 nc.scalar.activation(
-                    out=th[c, w][:, t, :], in_=acc[:, t - t0, :], func=ACT.Tanh, bias=bh[:, at : at + 1], scale=0.5
+                    out=th[c, w][:, t, :], in_=acc[:, t - t0, :], func=ACT.Tanh, bias=halves[:, t, w : w + 1], scale=0.5
                 )
 
         qg = {}
@@ -261,7 +261,7 @@ def tile_switchtabmutualsalientswap_d2p_kernel(tc, x_bytes, x_scale, p, b, g, wd
             engine.tensor_tensor(
                 out=qg[c][:, w, T4 * n0 : T4 * n1].rearrange("q (n i t) -> q n t i", i=2, t=T4),
                 in0=th[c, w][:, :, n0:n1].rearrange("q t (n i) -> q n t i", i=2),
-                in1=factor[:, T4 * w : T4 * (w + 1)].unsqueeze(1).unsqueeze(3).to_broadcast([P, (n1 - n0) // 2, T4, 2]),
+                in1=factor[:, :, 2 + w : 3 + w].unsqueeze(1).to_broadcast([P, (n1 - n0) // 2, T4, 2]),
                 op=MULT,
             )
 
@@ -320,14 +320,15 @@ def tile_switchtabmutualsalientswap_d2p_kernel(tc, x_bytes, x_scale, p, b, g, wd
         turn(0, 1, 2, ps_dec, "dec2")
         lay_p(0, 0, "v")
         lay_p(0, 2, "t", "dec3")
+        turn_rows()
         scale_out(0, 0, "s")
         scale_out(0, 1, "s")
-        halve(bh, braw)
         widen_scaled(1, 0, "s")
         quant_p(0, 0, 2)
         quant_x(0)
         widen_scaled(1, 1, "v")
         empty_p(0, 2)
+        copy_rows()
         project(0, 0, 0)
         lay_p(1, 2, "t", "dec0")
         turn(1, 0, 2, ps_dec, "dec1")
@@ -335,14 +336,12 @@ def tile_switchtabmutualsalientswap_d2p_kernel(tc, x_bytes, x_scale, p, b, g, wd
         quant_p(0, 2, 4)
         project(0, 0, 2)
         squash(0, 0, 0)
-        halve(gh, graw)
         empty_p(1, 2)
         widen_scaled(2, 0, "v")
         widen_scaled(2, 1, "v")
         quant_p(1, 0, 2)
         quant_p(1, 2, 4)
         copy_x(1, "s")
-        gain_to_psum()
         project(0, 1, 0)
         squash(0, 0, 2)
         project(0, 1, 2)

@@ -105,7 +105,7 @@ def tile_switchtabmutualsalientswap_d2p_kernel(tc, x_bytes, x_scale, p, b, g, wd
         nc.sync.dma_start(out=bdt[:], in_=bd.partition_broadcast(P))
 
         xs = kept([P, V + V * 16], F32, "xs")
-        halves = kept([P, T4, 4], F32, "halves")
+        halves = kept([P, 4, T4], F32, "halves")
         held = {}
 
         def spread_scales():
@@ -113,12 +113,12 @@ def tile_switchtabmutualsalientswap_d2p_kernel(tc, x_bytes, x_scale, p, b, g, wd
             nc.tensor.matmul(out=bank[:], lhsT=blocks[:], rhs=xs_rows[:], start=True, stop=True)
             nc.scalar.copy(out=xs[:], in_=bank[:])
 
-        gp = ps_g.tile([P, T4, 4], F32, name="gp")
+        gp = ps_g.tile([P, 4, T4], F32, name="gp")
         gh = halves
 
         def turn_rows():
             for t in range(T4):
-                nc.tensor.matmul(out=gp[:, t, :], lhsT=bg_rows[:, t:H:T4], rhs=halfb[:, 0:4], start=True, stop=True)
+                nc.tensor.matmul(out=gp[:, :, t], lhsT=bg_rows[:, t:H:T4], rhs=halfb[:, 0:4], start=True, stop=True)
 
         def copy_rows():
             nc.scalar.copy(out=halves[:], in_=gp[:])
@@ -205,9 +205,9 @@ def tile_switchtabmutualsalientswap_d2p_kernel(tc, x_bytes, x_scale, p, b, g, wd
             dst = pg[w][:].rearrange("q (t m j) -> q t m j", t=T4, j=T4)[:, t0 : t0 + count]
             src = praw[w][:].rearrange("q j (m t) -> q t m j", t=T4)[:, t0 : t0 + count]
             if engine == "v":
-                nc.vector.tensor_copy(out=dst, in_=src)
-            elif engine == "s":
-                nc.scalar.copy(out=dst, in_=src)
+                nc.vector.tensor_copy(
+                    out=dst.rearrange("q t (m i) j -> q m t i j", i=2), in_=src.rearrange("q t (m i) j -> q m t i j", i=2)
+                )
             else:
                 bank = ps_dec.tile([P, 2, P * T4], BF16, name=label)
                 for t in range(2):
@@ -244,12 +244,12 @@ def tile_switchtabmutualsalientswap_d2p_kernel(tc, x_bytes, x_scale, p, b, g, wd
 
         def squash(c, w, t0):
             if t0 == 0:
-                made = work.tile([P, T4, N], F32, name="th", bufs=4)
+                made = work.tile([P, T4, N], F32, name="th", bufs=8)
                 th[c, w] = made
             acc = held["proj", c, w, t0]
             for t in range(t0, t0 + 2):
                 nc.scalar.activation(
-                    out=th[c, w][:, t, :], in_=acc[:, t - t0, :], func=ACT.Tanh, bias=halves[:, t, w : w + 1], scale=0.5
+                    out=th[c, w][:, t, :], in_=acc[:, t - t0, :], func=ACT.Tanh, bias=halves[:, w, t : t + 1], scale=0.5
                 )
 
         qg = {}
@@ -258,10 +258,11 @@ def tile_switchtabmutualsalientswap_d2p_kernel(tc, x_bytes, x_scale, p, b, g, wd
             if c not in qg:
                 made = work.tile([P, 2, N * T4], BF16, name="qg", align_bytes=64, bufs=1)
                 qg[c] = made
+            run = 2 if factor is gp else 1
             engine.tensor_tensor(
-                out=qg[c][:, w, T4 * n0 : T4 * n1].rearrange("q (n i t) -> q n t i", i=2, t=T4),
-                in0=th[c, w][:, :, n0:n1].rearrange("q t (n i) -> q n t i", i=2),
-                in1=factor[:, :, 2 + w : 3 + w].unsqueeze(1).to_broadcast([P, (n1 - n0) // 2, T4, 2]),
+                out=qg[c][:, w, T4 * n0 : T4 * n1].rearrange("q (n i t) -> q n t i", i=run, t=T4),
+                in0=th[c, w][:, :, n0:n1].rearrange("q t (n i) -> q n t i", i=run),
+                in1=factor[:, 2 + w, :].unsqueeze(1).unsqueeze(3).to_broadcast([P, (n1 - n0) // run, T4, run]),
                 op=MULT,
             )
 
@@ -270,8 +271,8 @@ def tile_switchtabmutualsalientswap_d2p_kernel(tc, x_bytes, x_scale, p, b, g, wd
 
         def quant_q(c, w0, w1):
             if w0 == 0:
-                codes = work.tile([P, 2 * N], U32, name="qc", align_bytes=64)
-                scales = work.tile([P, 2 * N], U8, name="qs", align_bytes=64)
+                codes = work.tile([P, 2 * N], U32, name="qc", align_bytes=64, bufs=4)
+                scales = work.tile([P, 2 * N], U8, name="qs", align_bytes=64, bufs=4)
                 qc[c] = codes
                 qs[c] = scales
             cols = slice(N * w0, N * w1)
@@ -301,13 +302,13 @@ def tile_switchtabmutualsalientswap_d2p_kernel(tc, x_bytes, x_scale, p, b, g, wd
         zs = {}
 
         def add_bias(c, j):
-            if j % 2 == 0:
-                made = work.tile([P, 2, O], F32, name="z", bufs=4)
+            if (c, j // 2) not in zs:
+                made = work.tile([P, 2, O], F32, name="z", bufs=8)
                 zs[c, j // 2] = made
             nc.vector.tensor_tensor(out=zs[c, j // 2][:, j % 2, :], in0=held["dec", c, j][:], in1=bdt[:], op=ADD)
 
         def finish(c, j0, count):
-            y = work.tile([P, 2, O], F32, name="y", bufs=8)
+            y = work.tile([P, 2, O], F32, name="y", bufs=11)
             nc.scalar.activation(out=y[:, 0:count, :], in_=zs[c, j0 // 2][:, j0 % 2 : j0 % 2 + count, :], func=ACT.Sigmoid)
             nc.sync.dma_start(
                 out=out[j0 : j0 + count, P * c : P * (c + 1), :].rearrange("j q o -> q j o"), in_=y[:, 0:count, :]
@@ -346,13 +347,10 @@ def tile_switchtabmutualsalientswap_d2p_kernel(tc, x_bytes, x_scale, p, b, g, wd
         squash(0, 0, 2)
         project(0, 1, 2)
         turn(2, 0, 2, ps_dec, "dec2")
-        widen_scaled(3, 0, "v")
         quant_x(1)
-        widen_scaled(3, 1, "v")
         gain(0, 0, nc.vector, gp)
         squash(0, 1, 0)
         project(1, 0, 0)
-        turn(3, 0, 2, ps_dec, "dec3")
         squash(0, 1, 2)
         project(1, 0, 2)
         copy_x(2, "s")
@@ -370,11 +368,14 @@ def tile_switchtabmutualsalientswap_d2p_kernel(tc, x_bytes, x_scale, p, b, g, wd
         project(2, 0, 2)
         decode(0, 0, "dec0")
         decode(0, 1, "dec1")
-        copy_x(3, "v")
+        widen_scaled(3, 0, "s")
+        widen_scaled(3, 1, "s")
         gain(1, 1, nc.vector, gp)
+        turn(3, 0, 2, ps_dec, "dec3")
         squash(2, 0, 0)
         project(2, 1, 0)
         decode(0, 2, "dec2")
+        copy_x(3, "s")
         squash(2, 0, 2)
         project(2, 1, 2)
         decode(0, 3, "dec3")

@@ -64,8 +64,6 @@ def tile_switchtabmutualsalientswap_d2p_kernel(tc, x_bytes, x_scale, p, b, g, wd
         wds = kept([P, 2, O], U8, "wds")
         nc.vector.memset(wds[:].rearrange("q g n -> q (g n)").bitcast(I32), 0)
 
-        identb = kept([P, P], BF16, "identb")
-        nc.vector.tensor_copy(out=identb[:], in_=ident[:])
         halfb = kept([P, P], BF16, "halfb")
         nc.vector.tensor_scalar(out=halfb[:], in0=ident[:], scalar1=0.5, scalar2=None, op0=MULT)
 
@@ -160,6 +158,13 @@ def tile_switchtabmutualsalientswap_d2p_kernel(tc, x_bytes, x_scale, p, b, g, wd
             else:
                 nc.scalar.copy(out=dst, in_=src)
 
+        def copy_half(c, a, engine):
+            if c not in xg:
+                made = work.tile([P, V, P * T4], BF16, name="xg", align_bytes=64, bufs=4)
+                xg[c] = made
+            dst = xg[c][:, a, :].bitcast(F32).rearrange("q (r u) -> q r u", u=2)
+            nc.scalar.copy(out=dst, in_=held["xt", c, a].rearrange("q u r -> q r u"))
+
         def turn(c, a0=0, a1=V, pool=ps_proj, label="proj"):
             bank = pool.tile([P, a1 - a0, 2, P], F32, name=label)
             for a in range(a0, a1):
@@ -208,16 +213,6 @@ def tile_switchtabmutualsalientswap_d2p_kernel(tc, x_bytes, x_scale, p, b, g, wd
                 nc.vector.tensor_copy(
                     out=dst.rearrange("q t (m i) j -> q m t i j", i=2), in_=src.rearrange("q t (m i) j -> q m t i j", i=2)
                 )
-            else:
-                bank = ps_dec.tile([P, 2, P * T4], BF16, name=label)
-                for t in range(2):
-                    nc.tensor.matmul(out=bank[:, t, :], lhsT=identb[:], rhs=src[:, t], start=True, stop=True)
-                held["pt", w, t0] = bank
-
-        def empty_p(w, t0):
-            nc.scalar.copy(
-                out=pg[w][:, T4 * P * t0 : T4 * P * (t0 + 2)], in_=held["pt", w, t0][:].rearrange("q t n -> q (t n)")
-            )
 
         def quant_p(w, t0, t1):
             cols = slice(P * t0, P * t1)
@@ -319,40 +314,41 @@ def tile_switchtabmutualsalientswap_d2p_kernel(tc, x_bytes, x_scale, p, b, g, wd
         widen(0, "v", 1, 2)
         turn(0, 0, 1, ps_dec, "dec1")
         turn(0, 1, 2, ps_dec, "dec2")
-        lay_p(0, 0, "v")
-        lay_p(0, 2, "t", "dec3")
         turn_rows()
+        lay_p(0, 0, "v")
+        lay_p(0, 2, "v")
         scale_out(0, 0, "s")
         scale_out(0, 1, "s")
         widen_scaled(1, 0, "s")
+        widen_scaled(1, 1, "s")
+        copy_rows()
         quant_p(0, 0, 2)
         quant_x(0)
-        widen_scaled(1, 1, "v")
-        empty_p(0, 2)
-        copy_rows()
-        project(0, 0, 0)
-        lay_p(1, 2, "t", "dec0")
-        turn(1, 0, 2, ps_dec, "dec1")
-        lay_p(1, 0, "v")
         quant_p(0, 2, 4)
+        project(0, 0, 0)
         project(0, 0, 2)
+        lay_p(1, 0, "v")
+        lay_p(1, 2, "v")
+        widen_scaled(2, 0, "s")
+        turn(1, 0, 2, ps_dec, "dec1")
         squash(0, 0, 0)
-        empty_p(1, 2)
-        widen_scaled(2, 0, "v")
-        widen_scaled(2, 1, "v")
-        quant_p(1, 0, 2)
-        quant_p(1, 2, 4)
-        copy_x(1, "s")
-        project(0, 1, 0)
         squash(0, 0, 2)
+        quant_p(1, 0, 2)
+        project(0, 1, 0)
+        widen_scaled(2, 1, "v")
+        quant_p(1, 2, 4)
         project(0, 1, 2)
+        copy_x(1, "s")
         turn(2, 0, 2, ps_dec, "dec2")
+        widen_scaled(3, 0, "v")
         quant_x(1)
+        widen_scaled(3, 1, "v")
         gain(0, 0, nc.vector, gp)
         squash(0, 1, 0)
         project(1, 0, 0)
         squash(0, 1, 2)
         project(1, 0, 2)
+        turn(3, 0, 2, ps_dec, "dec3")
         copy_x(2, "s")
         gain(0, 1, nc.vector, gp)
         squash(1, 0, 0)
@@ -368,14 +364,11 @@ def tile_switchtabmutualsalientswap_d2p_kernel(tc, x_bytes, x_scale, p, b, g, wd
         project(2, 0, 2)
         decode(0, 0, "dec0")
         decode(0, 1, "dec1")
-        widen_scaled(3, 0, "s")
-        widen_scaled(3, 1, "s")
+        copy_x(3, "v")
         gain(1, 1, nc.vector, gp)
-        turn(3, 0, 2, ps_dec, "dec3")
         squash(2, 0, 0)
         project(2, 1, 0)
         decode(0, 2, "dec2")
-        copy_x(3, "s")
         squash(2, 0, 2)
         project(2, 1, 2)
         decode(0, 3, "dec3")

@@ -303,7 +303,7 @@ def tile_switchtabmutualsalientswap_d2p_kernel(tc, x_bytes, x_scale, p, b, g, wd
             nc.vector.tensor_tensor(out=zs[c, j // 2][:, j % 2, :], in0=held["dec", c, j][:], in1=bdt[:], op=ADD)
 
         def finish(c, j0, count):
-            y = work.tile([P, 2, O], F32, name="y", bufs=11)
+            y = work.tile([P, count, O], F32, name="y", bufs=14)
             nc.scalar.activation(out=y[:, 0:count, :], in_=zs[c, j0 // 2][:, j0 % 2 : j0 % 2 + count, :], func=ACT.Sigmoid)
             nc.sync.dma_start(
                 out=out[j0 : j0 + count, P * c : P * (c + 1), :].rearrange("j q o -> q j o"), in_=y[:, 0:count, :]
@@ -388,14 +388,16 @@ def tile_switchtabmutualsalientswap_d2p_kernel(tc, x_bytes, x_scale, p, b, g, wd
         add_bias(0, 3)
         decode(1, 2, "dec2")
         decode(1, 3, "dec3")
-        finish(0, 0, 2)
+        add_bias(1, 0)
         gain(2, 1, nc.vector, gp)
+        add_bias(1, 1)
+        finish(0, 0, 2)
         squash(3, 0, 0)
+        finish(0, 2, 2)
         project(3, 1, 2)
         squash(3, 0, 2)
-        finish(0, 2, 2)
-        add_bias(1, 0)
-        add_bias(1, 1)
+        finish(1, 0, 1)
+        finish(1, 1, 1)
         quant_q(2, 0, 2)
         gain(3, 0, nc.gpsimd, gh)
         decode(2, 0, "dec0")
@@ -404,14 +406,15 @@ def tile_switchtabmutualsalientswap_d2p_kernel(tc, x_bytes, x_scale, p, b, g, wd
         add_bias(1, 3)
         squash(3, 1, 0)
         squash(3, 1, 2)
-        finish(1, 0, 2)
-        finish(1, 2, 2)
+        finish(1, 2, 1)
+        finish(1, 3, 1)
         add_bias(2, 0)
         add_bias(2, 1)
         decode(2, 2, "dec0")
         decode(2, 3, "dec1")
         gain(3, 1, nc.vector, gp)
-        finish(2, 0, 2)
+        finish(2, 0, 1)
+        finish(2, 1, 1)
         quant_q(3, 0, 1)
         quant_q(3, 1, 2)
         decode(3, 0, "dec2")

@@ -211,7 +211,7 @@ def tile_switchtabmutualsalientswap_d2p_kernel(tc, x_bytes, x_scale, p, b, g, wd
             src = praw[w][:].rearrange("q j (m t) -> q t m j", t=T4)[:, t0 : t0 + count]
             if engine == "v":
                 nc.vector.tensor_copy(
-                    out=dst.rearrange("q t (m i) j -> q m t i j", i=2), in_=src.rearrange("q t (m i) j -> q m t i j", i=2)
+                    out=dst.rearrange("q t (m i) j -> q m t j i", i=2), in_=src.rearrange("q t (m i) j -> q m t j i", i=2)
                 )
 
         def quant_p(w, t0, t1):

@@ -48,10 +48,10 @@ def tile_switchtabmutualsalientswap_d2p_kernel(tc, x_bytes, x_scale, p, b, g, wd
         bg_rows = kept([P, H], BF16, "bg_rows")
         nc.vector.memset(bg_rows[:], 0.0)
 
-        warm = kept([P, 1], F32, "warm")
-        nc.vector.memset(warm[:], 0.0)
+        zeros = kept([P, 1], F32, "zeros")
+        nc.vector.memset(zeros[:], 0.0)
         warmed = kept([P, 1], F32, "warmed")
-        nc.scalar.activation(out=warmed[:], in_=warm[:], func=ACT.Sigmoid)
+        nc.scalar.activation(out=warmed[:], in_=zeros[:, 0:1], func=ACT.Sigmoid)
 
         ident = kept([P, P], F32, "ident")
         nc.vector.memset(ident[:], 0.0)
@@ -64,8 +64,9 @@ def tile_switchtabmutualsalientswap_d2p_kernel(tc, x_bytes, x_scale, p, b, g, wd
         wds = kept([P, 2, O], U8, "wds")
         nc.vector.memset(wds[:].rearrange("q g n -> q (g n)").bitcast(I32), 0)
 
-        halfb = kept([P, P], BF16, "halfb")
-        nc.vector.tensor_scalar(out=halfb[:], in0=ident[:], scalar1=0.5, scalar2=None, op0=MULT)
+        pick = kept([P, 8], BF16, "pick")
+        nc.vector.tensor_scalar(out=pick[:, 0:4], in0=ident[:, 0:4], scalar1=0.5, scalar2=None, op0=MULT)
+        nc.vector.tensor_copy(out=pick[:, 4:8], in_=ident[:, 4:8])
 
         xb = {}
 
@@ -88,6 +89,7 @@ def tile_switchtabmutualsalientswap_d2p_kernel(tc, x_bytes, x_scale, p, b, g, wd
         load_p(0)
         nc.sync.dma_start(out=bg_rows[0:2, :], in_=b)
         nc.sync.dma_start(out=bg_rows[2:4, :], in_=g.rearrange("(w c) -> w c", w=2))
+        nc.sync.dma_start(out=bg_rows[4:5, :], in_=bd.rearrange("(w c) -> w c", w=1))
         load_x(1)
         load_p(1)
         load_x(2)
@@ -103,7 +105,7 @@ def tile_switchtabmutualsalientswap_d2p_kernel(tc, x_bytes, x_scale, p, b, g, wd
         nc.sync.dma_start(out=bdt[:], in_=bd.partition_broadcast(P))
 
         xs = kept([P, V + V * 16], F32, "xs")
-        halves = kept([P, 4, T4], F32, "halves")
+        halves = kept([P, 5, T4], F32, "halves")
         held = {}
 
         def spread_scales():
@@ -111,17 +113,27 @@ def tile_switchtabmutualsalientswap_d2p_kernel(tc, x_bytes, x_scale, p, b, g, wd
             nc.tensor.matmul(out=bank[:], lhsT=blocks[:], rhs=xs_rows[:], start=True, stop=True)
             nc.scalar.copy(out=xs[:], in_=bank[:])
 
-        gp = ps_g.tile([P, 4, T4], F32, name="gp")
+        gp = ps_g.tile([P, 5, T4], F32, name="gp")
         gh = halves
 
         def turn_rows():
             for t in range(T4):
-                nc.tensor.matmul(out=gp[:, :, t], lhsT=bg_rows[:, t:H:T4], rhs=halfb[:, 0:4], start=True, stop=True)
+                nc.tensor.matmul(out=gp[:, 0:4, t], lhsT=bg_rows[:, t:H:T4], rhs=pick[:, 0:4], start=True, stop=True)
+
+        def turn_bd():
+            for r in range(O // P):
+                nc.tensor.matmul(out=gp[:, 4:5, r], lhsT=bg_rows[:, P * r : P * (r + 1)], rhs=pick[:, 4:5], start=True, stop=True)
 
         def copy_rows():
-            nc.scalar.copy(out=halves[:], in_=gp[:])
+            nc.scalar.copy(out=halves[:, 0:4, :], in_=gp[:, 0:4, :])
+
+        def copy_bd():
+            nc.scalar.copy(out=halves[:, 4, :], in_=gp[:, 4, :])
 
         xw = {}
+        parted = set()
+        one = kept([P, 1], F32, "one")
+        nc.vector.memset(one[:], 1.0)
         xg = {}
 
         def widen(c, engine, a0=0, a1=V):
@@ -130,10 +142,9 @@ def tile_switchtabmutualsalientswap_d2p_kernel(tc, x_bytes, x_scale, p, b, g, wd
                 xw[c] = made
             cols = slice(D * a0, D * a1)
             src = xb[c][:].rearrange("q a k -> q (a k)")[:, cols].bitcast(FP8)
-            if engine == "v":
-                nc.vector.tensor_copy(out=xw[c][:, cols], in_=src)
-            else:
-                nc.scalar.copy(out=xw[c][:, cols], in_=src)
+            dst = xw[c][:, cols].rearrange("q (u m e) -> q m u e", u=2, e=2)
+            nc.vector.tensor_scalar(out=dst, in0=src.rearrange("q (m u e) -> q m u e", u=2, e=2), scalar1=one[:], scalar2=None, op0=MULT)
+            parted.add((c, a0))
 
         def widen_scaled(c, a, engine):
             if c not in xw:
@@ -144,12 +155,15 @@ def tile_switchtabmutualsalientswap_d2p_kernel(tc, x_bytes, x_scale, p, b, g, wd
                 at = 16 * a + 4 * c + j
                 src = xb[c][:].rearrange("q a k -> q (a k)")[:, cols].bitcast(FP8)
                 if engine == "v":
-                    nc.vector.tensor_scalar(out=xw[c][:, cols], in0=src, scalar1=xs[:, at : at + 1], scalar2=None, op0=MULT)
+                    dst = xw[c][:, D * a : D * (a + 1)].rearrange("q (u m e) -> q m u e", u=2, e=2)[:, 32 * j : 32 * (j + 1)]
+                    src = src.rearrange("q (m u e) -> q m u e", u=2, e=2)
+                    nc.vector.tensor_scalar(out=dst, in0=src, scalar1=xs[:, at : at + 1], scalar2=None, op0=MULT)
+                    parted.add((c, a))
                 else:
                     nc.scalar.activation(out=xw[c][:, cols], in_=src, func=ACT.Copy, scale=xs[:, at : at + 1])
 
-        def copy_x(c, engine):
-            made = work.tile([P, V, P * T4], BF16, name="xg", align_bytes=64, bufs=4)
+        def copy_x(c, engine, label):
+            made = work.tile([P, V, P * T4], BF16, name=label, align_bytes=64, bufs=1)
             xg[c] = made
             dst = made[:].bitcast(F32).rearrange("q a (r u) -> q a r u", u=2)
             src = held["xtb", c][:].rearrange("q a u r -> q a r u")
@@ -170,7 +184,8 @@ def tile_switchtabmutualsalientswap_d2p_kernel(tc, x_bytes, x_scale, p, b, g, wd
             for a in range(a0, a1):
                 words = xw[c][:, D * a : D * (a + 1)].bitcast(F32)
                 for u in range(2):
-                    nc.tensor.transpose(bank[:, a - a0, u, :], words[:, u : D // 2 : 2], ident[:])
+                    half = words[:, P * u : P * (u + 1)] if (c, a) in parted else words[:, u : D // 2 : 2]
+                    nc.tensor.transpose(bank[:, a - a0, u, :], half, ident[:])
                 held["xt", c, a] = bank[:, a - a0, :, :]
             held["xtb", c] = bank
 
@@ -250,12 +265,12 @@ def tile_switchtabmutualsalientswap_d2p_kernel(tc, x_bytes, x_scale, p, b, g, wd
         qg = {}
 
         def gain(c, w, engine, factor, n0=0, n1=N):
-            if c not in qg:
-                made = work.tile([P, 2, N * T4], BF16, name="qg", align_bytes=64, bufs=1)
-                qg[c] = made
+            if (c, w) not in qg:
+                made = work.tile([P, N * T4], BF16, name="qg%d" % ((c + w) % 2), align_bytes=64, bufs=1)
+                qg[c, w] = made
             run = 2 if factor is gp else 1
             engine.tensor_tensor(
-                out=qg[c][:, w, T4 * n0 : T4 * n1].rearrange("q (n i t) -> q n t i", i=run, t=T4),
+                out=qg[c, w][:, T4 * n0 : T4 * n1].rearrange("q (n i t) -> q n t i", i=run, t=T4),
                 in0=th[c, w][:, :, n0:n1].rearrange("q t (n i) -> q n t i", i=run),
                 in1=factor[:, 2 + w, :].unsqueeze(1).unsqueeze(3).to_broadcast([P, (n1 - n0) // run, T4, run]),
                 op=MULT,
@@ -264,18 +279,14 @@ def tile_switchtabmutualsalientswap_d2p_kernel(tc, x_bytes, x_scale, p, b, g, wd
         qc = {}
         qs = {}
 
-        def quant_q(c, w0, w1):
-            if w0 == 0:
+        def quant_q(c, w):
+            if c not in qc:
                 codes = work.tile([P, 2 * N], U32, name="qc", align_bytes=64, bufs=4)
                 scales = work.tile([P, 2 * N], U8, name="qs", align_bytes=64, bufs=4)
                 qc[c] = codes
                 qs[c] = scales
-            cols = slice(N * w0, N * w1)
-            nc.vector.quantize_mx(
-                out=qc[c][:, cols].bitcast(FP8X4),
-                scales=qs[c][:, cols],
-                in_=qg[c][:, w0:w1, :].rearrange("q w n -> q (w n)"),
-            )
+            cols = slice(N * w, N * (w + 1))
+            nc.vector.quantize_mx(out=qc[c][:, cols].bitcast(FP8X4), scales=qs[c][:, cols], in_=qg[c, w][:])
 
         def decode(c, j, label, pool=ps_dec, w0=0, w1=2):
             if w0 == 0:
@@ -309,6 +320,42 @@ def tile_switchtabmutualsalientswap_d2p_kernel(tc, x_bytes, x_scale, p, b, g, wd
                 out=out[j0 : j0 + count, P * c : P * (c + 1), :].rearrange("j q o -> q j o"), in_=y[:, 0:count, :]
             )
 
+        yt = {}
+
+        def decode_turned(c, j, label, pool=ps_dec):
+            acc = pool.tile([P, O // P, P], F32, name=label)
+            held["dect", c, j] = acc
+            for r in range(O // P):
+                for w in range(2):
+                    at = N * w + P * PARTS[j][w]
+                    nc.tensor.matmul_mx(
+                        out=acc[:, r, :],
+                        lhsT=wdw[:, w, 2 * P * r : 2 * P * (r + 1)].bitcast(FP4X4),
+                        lhsT_scale=wds[:, w, P * r : P * (r + 1)],
+                        rhs=qc[c][:, at : at + P].bitcast(FP8X4),
+                        rhs_scale=qs[c][:, at : at + P],
+                        start=(w == 0),
+                        stop=(w == 1),
+                    )
+
+        def finish_turned(c, j):
+            yt[c, j] = kept([P, O // P, P], F32, "yt%d%d" % (c, j))
+            for r in range(O // P):
+                nc.scalar.activation(
+                    out=yt[c, j][:, r, :], in_=held["dect", c, j][:, r, :], func=ACT.Sigmoid, bias=halves[:, 4, r : r + 1]
+                )
+
+        def turn_back(c, j, label, pool=ps_dec):
+            bank = pool.tile([P, O], F32, name=label)
+            held["back", c, j] = bank
+            for r in range(O // P):
+                nc.tensor.transpose(bank[:, P * r : P * (r + 1)], yt[c, j][:, r, :], ident[:])
+
+        def store_turned(c, j):
+            y = kept([P, O], F32, "turned%d%d" % (c, j))
+            nc.scalar.copy(out=y[:], in_=held["back", c, j][:])
+            nc.sync.dma_start(out=out[j, P * c : P * (c + 1), :], in_=y[:])
+
         spread_scales()
         widen(0, "v", 0, 1)
         widen(0, "v", 1, 2)
@@ -338,89 +385,94 @@ def tile_switchtabmutualsalientswap_d2p_kernel(tc, x_bytes, x_scale, p, b, g, wd
         widen_scaled(2, 1, "v")
         quant_p(1, 2, 4)
         project(0, 1, 2)
-        copy_x(1, "s")
+        copy_x(1, "s", "qg0")
         turn(2, 0, 2, ps_dec, "dec2")
         widen_scaled(3, 0, "v")
-        quant_x(1)
         widen_scaled(3, 1, "v")
-        gain(0, 0, nc.vector, gp)
+        quant_x(1)
+        gain(0, 0, nc.gpsimd, gh)
+        copy_x(2, "v", "xg2")
         squash(0, 1, 0)
         project(1, 0, 0)
         squash(0, 1, 2)
         project(1, 0, 2)
         turn(3, 0, 2, ps_dec, "dec3")
-        copy_x(2, "s")
         gain(0, 1, nc.vector, gp)
+        copy_x(3, "v", "xg3")
         squash(1, 0, 0)
         project(1, 1, 0)
         squash(1, 0, 2)
         project(1, 1, 2)
+        turn_bd()
         quant_x(2)
-        quant_q(0, 0, 2)
+        quant_q(0, 0)
+        quant_x(3)
+        quant_q(0, 1)
         gain(1, 0, nc.gpsimd, gh)
         squash(1, 1, 0)
         project(2, 0, 0)
         squash(1, 1, 2)
+        copy_bd()
         project(2, 0, 2)
+        project(2, 1, 0)
         decode(0, 0, "dec0")
         decode(0, 1, "dec1")
-        copy_x(3, "v")
         gain(1, 1, nc.vector, gp)
         squash(2, 0, 0)
-        project(2, 1, 0)
+        project(2, 1, 2)
         decode(0, 2, "dec2")
         squash(2, 0, 2)
-        project(2, 1, 2)
+        project(3, 0, 0)
         decode(0, 3, "dec3")
         add_bias(0, 0)
         add_bias(0, 1)
-        quant_x(3)
-        quant_q(1, 0, 2)
-        gain(2, 0, nc.gpsimd, gh)
+        add_bias(0, 2)
         squash(2, 1, 0)
-        squash(2, 1, 2)
-        project(3, 0, 0)
         project(3, 0, 2)
+        squash(2, 1, 2)
+        project(3, 1, 0)
+        quant_q(1, 1)
+        quant_q(1, 0)
+        gain(2, 0, nc.gpsimd, gh)
         decode(1, 0, "dec0")
         decode(1, 1, "dec1")
-        project(3, 1, 0)
-        add_bias(0, 2)
         add_bias(0, 3)
-        decode(1, 2, "dec2")
-        decode(1, 3, "dec3")
-        add_bias(1, 0)
-        gain(2, 1, nc.vector, gp)
-        add_bias(1, 1)
         finish(0, 0, 2)
         squash(3, 0, 0)
-        finish(0, 2, 2)
         project(3, 1, 2)
+        decode(1, 2, "dec2")
+        decode_turned(1, 3, "dec3")
+        gain(2, 1, nc.vector, gp)
+        add_bias(1, 0)
+        add_bias(1, 1)
         squash(3, 0, 2)
-        finish(1, 0, 1)
-        finish(1, 1, 1)
-        quant_q(2, 0, 2)
+        finish(0, 2, 2)
+        squash(3, 1, 0)
+        squash(3, 1, 2)
+        finish(1, 0, 2)
+        finish_turned(1, 3)
+        quant_q(2, 1)
+        quant_q(2, 0)
         gain(3, 0, nc.gpsimd, gh)
         decode(2, 0, "dec0")
         decode(2, 1, "dec1")
+        decode(2, 2, "proj", ps_proj)
+        decode(2, 3, "proj", ps_proj)
         add_bias(1, 2)
-        add_bias(1, 3)
-        squash(3, 1, 0)
-        squash(3, 1, 2)
+        gain(3, 1, nc.vector, gp)
         finish(1, 2, 1)
-        finish(1, 3, 1)
         add_bias(2, 0)
         add_bias(2, 1)
-        decode(2, 2, "dec0")
-        decode(2, 3, "dec1")
-        gain(3, 1, nc.vector, gp)
+        turn_back(1, 3, "dec3")
         finish(2, 0, 1)
+        store_turned(1, 3)
         finish(2, 1, 1)
-        quant_q(3, 0, 1)
-        quant_q(3, 1, 2)
+        quant_q(3, 1)
+        quant_q(3, 0)
         decode(3, 0, "dec2")
-        decode(3, 1, "dec3")
-        decode(3, 2, "proj", ps_proj)
-        decode(3, 3, "proj", ps_proj)
+        decode(3, 1, "dec0")
+        decode(3, 2, "dec1")
+        decode(3, 3, "dec3")
         add_bias(2, 2)
         add_bias(2, 3)
         finish(2, 2, 1)

@@ -48,7 +48,7 @@ def tile_switchtabmutualsalientswap_d2p_kernel(tc, x_bytes, x_scale, p, b, g, wd
         bg_rows = kept([P, H], BF16, "bg_rows")
         nc.vector.memset(bg_rows[:], 0.0)
 
-        zeros = kept([P, 1], F32, "zeros")
+        zeros = kept([P, 2 * P], F32, "zeros")
         nc.vector.memset(zeros[:], 0.0)
         warmed = kept([P, 1], F32, "warmed")
         nc.scalar.activation(out=warmed[:], in_=zeros[:, 0:1], func=ACT.Sigmoid)
@@ -115,6 +115,10 @@ def tile_switchtabmutualsalientswap_d2p_kernel(tc, x_bytes, x_scale, p, b, g, wd
 
         gp = ps_g.tile([P, 5, T4], F32, name="gp")
         gh = halves
+
+        def warm_up(label):
+            bank = ps_proj.tile([P, 2 * P], F32, name=label)
+            nc.tensor.matmul(out=bank[:], lhsT=zeros[:, 0:P], rhs=zeros[:], start=True, stop=True)
 
         def turn_rows():
             for t in range(T4):
@@ -362,6 +366,7 @@ def tile_switchtabmutualsalientswap_d2p_kernel(tc, x_bytes, x_scale, p, b, g, wd
         turn(0, 0, 1, ps_dec, "dec1")
         turn(0, 1, 2, ps_dec, "dec2")
         turn_rows()
+        warm_up("proj")
         lay_p(0, 0, "v")
         lay_p(0, 2, "v")
         scale_out(0, 0, "s")

@@ -135,9 +135,6 @@ def tile_switchtabmutualsalientswap_d2p_kernel(tc, x_bytes, x_scale, p, b, g, wd
             nc.scalar.copy(out=halves[:, 4, :], in_=gp[:, 4, :])
 
         xw = {}
-        parted = set()
-        one = kept([P, 1], F32, "one")
-        nc.vector.memset(one[:], 1.0)
         xg = {}
 
         def widen(c, engine, a0=0, a1=V):
@@ -146,9 +143,7 @@ def tile_switchtabmutualsalientswap_d2p_kernel(tc, x_bytes, x_scale, p, b, g, wd
                 xw[c] = made
             cols = slice(D * a0, D * a1)
             src = xb[c][:].rearrange("q a k -> q (a k)")[:, cols].bitcast(FP8)
-            dst = xw[c][:, cols].rearrange("q (u m e) -> q m u e", u=2, e=2)
-            nc.vector.tensor_scalar(out=dst, in0=src.rearrange("q (m u e) -> q m u e", u=2, e=2), scalar1=one[:], scalar2=None, op0=MULT)
-            parted.add((c, a0))
+            nc.vector.tensor_copy(out=xw[c][:, cols], in_=src)
 
         def widen_scaled(c, a, engine):
             if c not in xw:
@@ -159,10 +154,7 @@ def tile_switchtabmutualsalientswap_d2p_kernel(tc, x_bytes, x_scale, p, b, g, wd
                 at = 16 * a + 4 * c + j
                 src = xb[c][:].rearrange("q a k -> q (a k)")[:, cols].bitcast(FP8)
                 if engine == "v":
-                    dst = xw[c][:, D * a : D * (a + 1)].rearrange("q (u m e) -> q m u e", u=2, e=2)[:, 32 * j : 32 * (j + 1)]
-                    src = src.rearrange("q (m u e) -> q m u e", u=2, e=2)
-                    nc.vector.tensor_scalar(out=dst, in0=src, scalar1=xs[:, at : at + 1], scalar2=None, op0=MULT)
-                    parted.add((c, a))
+                    nc.vector.tensor_scalar(out=xw[c][:, cols], in0=src, scalar1=xs[:, at : at + 1], scalar2=None, op0=MULT)
                 else:
                     nc.scalar.activation(out=xw[c][:, cols], in_=src, func=ACT.Copy, scale=xs[:, at : at + 1])
 
@@ -188,8 +180,7 @@ def tile_switchtabmutualsalientswap_d2p_kernel(tc, x_bytes, x_scale, p, b, g, wd
             for a in range(a0, a1):
                 words = xw[c][:, D * a : D * (a + 1)].bitcast(F32)
                 for u in range(2):
-                    half = words[:, P * u : P * (u + 1)] if (c, a) in parted else words[:, u : D // 2 : 2]
-                    nc.tensor.transpose(bank[:, a - a0, u, :], half, ident[:])
+                    nc.tensor.transpose(bank[:, a - a0, u, :], words[:, u : D // 2 : 2], ident[:])
                 held["xt", c, a] = bank[:, a - a0, :, :]
             held["xtb", c] = bank
 

@@ -43,7 +43,7 @@ def tile_switchtabmutualsalientswap_d2p_kernel(tc, x_bytes, x_scale, p, b, g, wd
             made = keep.tile(shape, dtype, name=label, align_bytes=64)
             return made
 
-        xs_rows = kept([P, V * 16 + V], F32, "xs_rows")
+        xs_rows = kept([P, V * 16 + V * 4], F32, "xs_rows")
         nc.vector.memset(xs_rows[:], 0.0)
         bg_rows = kept([P, H], BF16, "bg_rows")
         nc.vector.memset(bg_rows[:], 0.0)
@@ -84,7 +84,7 @@ def tile_switchtabmutualsalientswap_d2p_kernel(tc, x_bytes, x_scale, p, b, g, wd
 
         load_x(0)
         with nc.allow_non_contiguous_dma(reason="32 scales, turned on the way in"):
-            nc.sync.dma_start(out=xs_rows[0:P:32, V * 16 : V * 16 + V], in_=x_scale[:, 0, :].rearrange("a j -> j a"))
+            nc.sync.dma_start(out=xs_rows[0:P:32, V * 16 : V * 16 + V * 4], in_=x_scale.rearrange("a i j -> j (a i)"))
         nc.sync.dma_start(out=xs_rows[0:P:32, 0 : V * 16], in_=x_scale.rearrange("a i j -> (a i j)").partition_broadcast(4))
         load_p(0)
         nc.sync.dma_start(out=bg_rows[0:2, :], in_=b)
@@ -104,12 +104,12 @@ def tile_switchtabmutualsalientswap_d2p_kernel(tc, x_bytes, x_scale, p, b, g, wd
         bdt = kept([P, O], BF16, "bdt")
         nc.sync.dma_start(out=bdt[:], in_=bd.partition_broadcast(P))
 
-        xs = kept([P, V + V * 16], F32, "xs")
+        xs = kept([P, V * 4 + V * 16], F32, "xs")
         halves = kept([P, 5, T4], F32, "halves")
         held = {}
 
         def spread_scales():
-            bank = ps_dec.tile([P, V + V * 16], F32, name="dec0")
+            bank = ps_dec.tile([P, V * 4 + V * 16], F32, name="dec0")
             nc.tensor.matmul(out=bank[:], lhsT=blocks[:], rhs=xs_rows[:], start=True, stop=True)
             nc.scalar.copy(out=xs[:], in_=bank[:])
 
@@ -138,7 +138,7 @@ def tile_switchtabmutualsalientswap_d2p_kernel(tc, x_bytes, x_scale, p, b, g, wd
         xg = {}
 
         def widen(c, engine, a0=0, a1=V):
-            if a0 == 0:
+            if c not in xw:
                 made = work.tile([P, V * D], BF16, name="xw", align_bytes=64, bufs=4)
                 xw[c] = made
             cols = slice(D * a0, D * a1)
@@ -173,7 +173,7 @@ def tile_switchtabmutualsalientswap_d2p_kernel(tc, x_bytes, x_scale, p, b, g, wd
                 made = work.tile([P, V, P * T4], BF16, name="xg", align_bytes=64, bufs=4)
                 xg[c] = made
             dst = xg[c][:, a, :].bitcast(F32).rearrange("q (r u) -> q r u", u=2)
-            nc.scalar.copy(out=dst, in_=held["xt", c, a].rearrange("q u r -> q r u"))
+            nc.vector.tensor_copy(out=dst, in_=held["xt", c, a].rearrange("q u r -> q r u"))
 
         def turn(c, a0=0, a1=V, pool=ps_proj, label="proj"):
             bank = pool.tile([P, a1 - a0, 2, P], F32, name=label)
@@ -190,7 +190,7 @@ def tile_switchtabmutualsalientswap_d2p_kernel(tc, x_bytes, x_scale, p, b, g, wd
                 xg[c] = made
             src = held["xt", c, a].bitcast(BF16).rearrange("q u (r e) -> q r u e", e=2)
             dst = xg[c][:, a, :].rearrange("q (r u e) -> q r u e", u=2, e=2)
-            at = V * 16 + a
+            at = V * 16 + 4 * a + c
             if engine == "v":
                 nc.vector.tensor_scalar(out=dst, in0=src, scalar1=xs[:, at : at + 1], scalar2=None, op0=MULT)
             else:
@@ -378,23 +378,24 @@ def tile_switchtabmutualsalientswap_d2p_kernel(tc, x_bytes, x_scale, p, b, g, wd
         squash(0, 0, 2)
         quant_p(1, 0, 2)
         project(0, 1, 0)
-        widen_scaled(2, 1, "v")
+        widen(2, "v", 1, 2)
         quant_p(1, 2, 4)
         project(0, 1, 2)
         copy_x(1, "s", "qg0")
         turn(2, 0, 2, ps_dec, "dec2")
-        widen_scaled(3, 0, "v")
-        widen_scaled(3, 1, "v")
+        widen(3, "v")
         quant_x(1)
         gain(0, 0, nc.gpsimd, gh)
-        copy_x(2, "v", "xg2")
+        copy_half(2, 0, "v")
+        scale_out(2, 1, "v")
         squash(0, 1, 0)
         project(1, 0, 0)
         squash(0, 1, 2)
         project(1, 0, 2)
         turn(3, 0, 2, ps_dec, "dec3")
         gain(0, 1, nc.vector, gp)
-        copy_x(3, "v", "xg3")
+        scale_out(3, 0, "v")
+        scale_out(3, 1, "v")
         squash(1, 0, 0)
         project(1, 1, 0)
         squash(1, 0, 2)

@@ -24,6 +24,7 @@ H = 512
 O = 512
 CHUNKS = B // P
 N = V * P
+SHARE = 224
 PARTS = ((0, 0), (1, 1), (1, 0), (0, 1))
 
 FLOPS = 2 * (V * V * B * D * H + len(PARTS) * B * 2 * H * O)
@@ -362,9 +363,9 @@ def tile_switchtabmutualsalientswap_d2p_kernel(tc, x_bytes, x_scale, p, b, g, wd
         lay_p(0, 2, "v")
         scale_out(0, 0, "s")
         scale_out(0, 1, "s")
+        copy_rows()
         widen_scaled(1, 0, "s")
         widen_scaled(1, 1, "s")
-        copy_rows()
         quant_p(0, 0, 2)
         quant_x(0)
         quant_p(0, 2, 4)
@@ -372,21 +373,21 @@ def tile_switchtabmutualsalientswap_d2p_kernel(tc, x_bytes, x_scale, p, b, g, wd
         project(0, 0, 2)
         lay_p(1, 0, "v")
         lay_p(1, 2, "v")
-        widen_scaled(2, 0, "s")
         turn(1, 0, 2, ps_dec, "dec1")
         squash(0, 0, 0)
+        copy_x(1, "s", "qg0")
         squash(0, 0, 2)
         quant_p(1, 0, 2)
         project(0, 1, 0)
-        widen(2, "v", 1, 2)
         quant_p(1, 2, 4)
         project(0, 1, 2)
-        copy_x(1, "s", "qg0")
+        widen(2, "v")
         turn(2, 0, 2, ps_dec, "dec2")
-        widen(3, "v")
         quant_x(1)
-        gain(0, 0, nc.gpsimd, gh)
-        copy_half(2, 0, "v")
+        widen(3, "v")
+        gain(0, 0, nc.gpsimd, gh, 0, SHARE)
+        gain(0, 0, nc.vector, gp, SHARE, N)
+        scale_out(2, 0, "v")
         scale_out(2, 1, "v")
         squash(0, 1, 0)
         project(1, 0, 0)
@@ -402,9 +403,9 @@ def tile_switchtabmutualsalientswap_d2p_kernel(tc, x_bytes, x_scale, p, b, g, wd
         project(1, 1, 2)
         turn_bd()
         quant_x(2)
-        quant_q(0, 0)
         quant_x(3)
         quant_q(0, 1)
+        quant_q(0, 0)
         gain(1, 0, nc.gpsimd, gh)
         squash(1, 1, 0)
         project(2, 0, 0)

@@ -352,6 +352,7 @@ def tile_switchtabmutualsalientswap_d2p_kernel(tc, x_bytes, x_scale, p, b, g, wd
             nc.scalar.copy(out=y[:], in_=held["back", c, j][:])
             nc.sync.dma_start(out=out[j, P * c : P * (c + 1), :], in_=y[:])
 
+        warm_up("proj")
         spread_scales()
         widen(0, "v", 0, 1)
         widen(0, "v", 1, 2)

from contextlib import ExitStack

import concourse.mybir as mybir
from concourse.masks import make_identity

F32 = mybir.dt.float32
BF16 = mybir.dt.bfloat16
I32 = mybir.dt.int32
U32 = mybir.dt.uint32
U8 = mybir.dt.uint8
FP8 = mybir.dt.float8_e4m3fn
FP8X4 = mybir.dt.float8_e4m3fn_x4
FP4X4 = mybir.dt.float4_e2m1fn_x4
ACT = mybir.ActivationFunctionType
MULT = mybir.AluOpType.mult
ADD = mybir.AluOpType.add

P = 128
T4 = 4
V = 2
B = 512
D = 512
H = 512
O = 512
CHUNKS = B // P
N = V * P
SHARE = 224
PARTS = ((0, 0), (1, 1), (1, 0), (0, 1))

FLOPS = 2 * (V * V * B * D * H + len(PARTS) * B * 2 * H * O)


def tile_switchtabmutualsalientswap_d2p_kernel(tc, x_bytes, x_scale, p, b, g, wd_words, wd_scales, bd, out):
    nc = tc.nc
    with ExitStack() as ctx:
        keep = ctx.enter_context(tc.tile_pool(name="keep", bufs=1))
        work = ctx.enter_context(tc.tile_pool(name="work", bufs=2))
        ps_proj = ctx.enter_context(tc.psum_pool(name="ps_proj", bufs=3))
        ps_dec = ctx.enter_context(tc.psum_pool(name="ps_dec", bufs=1))
        ps_g = ctx.enter_context(tc.psum_pool(name="ps_g", bufs=1))
        ctx.enter_context(tc.manual_schedule())

        def kept(shape, dtype, label):
            made = keep.tile(shape, dtype, name=label, align_bytes=64)
            return made

        xs_rows = kept([P, V * 16 + V * 4], F32, "xs_rows")
        nc.vector.memset(xs_rows[:], 0.0)
        bg_rows = kept([P, H], BF16, "bg_rows")
        nc.vector.memset(bg_rows[:], 0.0)

        zeros = kept([P, 2 * P], F32, "zeros")
        nc.vector.memset(zeros[:], 0.0)
        warmed = kept([P, 1], F32, "warmed")
        nc.scalar.activation(out=warmed[:], in_=zeros[:, 0:1], func=ACT.Sigmoid)

        ident = kept([P, P], F32, "ident")
        nc.vector.memset(ident[:], 0.0)
        make_identity(nc, ident[:], nomemset=True)
        blocks = kept([P, P], F32, "blocks")
        nc.vector.memset(blocks[:], 0.0)
        for quad in range(4):
            rows = slice(32 * quad, 32 * (quad + 1))
            nc.vector.memset(blocks[rows, rows], 1.0)
        wds = kept([P, 2, O], U8, "wds")
        nc.vector.memset(wds[:].rearrange("q g n -> q (g n)").bitcast(I32), 0)

        pick = kept([P, 8], BF16, "pick")
        nc.vector.tensor_scalar(out=pick[:, 0:4], in0=ident[:, 0:4], scalar1=0.5, scalar2=None, op0=MULT)
        nc.vector.tensor_copy(out=pick[:, 4:8], in_=ident[:, 4:8])

        xb = {}

        def load_x(c):
            tile = kept([P, V, D], U8, "xb%d" % c)
            nc.sync.dma_start(out=tile[:], in_=x_bytes[:, P * c : P * (c + 1), :].rearrange("a q k -> q a k"))
            xb[c] = tile

        praw = {}

        def load_p(w):
            tile = kept([P, T4, H], BF16, "praw%d" % w)
            nc.sync.dma_start(out=tile[:], in_=p[w].rearrange("(q j) c -> q j c", j=T4))
            praw[w] = tile

        load_x(0)
        with nc.allow_non_contiguous_dma(reason="32 scales, turned on the way in"):
            nc.sync.dma_start(out=xs_rows[0:P:32, V * 16 : V * 16 + V * 4], in_=x_scale.rearrange("a i j -> j (a i)"))
        nc.sync.dma_start(out=xs_rows[0:P:32, 0 : V * 16], in_=x_scale.rearrange("a i j -> (a i j)").partition_broadcast(4))
        load_p(0)
        nc.sync.dma_start(out=bg_rows[0:2, :], in_=b)
        nc.sync.dma_start(out=bg_rows[2:4, :], in_=g.rearrange("(w c) -> w c", w=2))
        nc.sync.dma_start(out=bg_rows[4:5, :], in_=bd.rearrange("(w c) -> w c", w=1))
        load_x(1)
        load_p(1)
        load_x(2)
        load_x(3)
        wdw = kept([P, 2, 2 * O], U8, "wdw")
        nc.sync.dma_start(out=wdw[:].bitcast(I32), in_=wd_words.bitcast(I32).rearrange("g q n -> q g n"))
        for quad in range(4):
            nc.sync.dma_start(
                out=wds[32 * quad : 32 * quad + 4, :, :].bitcast(I32),
                in_=wd_scales[:, 4 * quad : 4 * quad + 4, :].bitcast(I32).rearrange("g q n -> q g n"),
            )
        bdt = kept([P, O], BF16, "bdt")
        nc.sync.dma_start(out=bdt[:], in_=bd.partition_broadcast(P))

        xs = kept([P, V * 4 + V * 16], F32, "xs")
        halves = kept([P, 5, T4], F32, "halves")
        held = {}

        def spread_scales():
            bank = ps_dec.tile([P, V * 4 + V * 16], F32, name="dec0")
            nc.tensor.matmul(out=bank[:], lhsT=blocks[:], rhs=xs_rows[:], start=True, stop=True)
            nc.scalar.copy(out=xs[:], in_=bank[:])

        gp = ps_g.tile([P, 5, T4], F32, name="gp")
        gh = halves

        def warm_up(label):
            bank = ps_proj.tile([P, 2 * P], F32, name=label)
            nc.tensor.matmul(out=bank[:], lhsT=zeros[:, 0:P], rhs=zeros[:], start=True, stop=True)

        def turn_rows():
            for t in range(T4):
                nc.tensor.matmul(out=gp[:, 0:4, t], lhsT=bg_rows[:, t:H:T4], rhs=pick[:, 0:4], start=True, stop=True)

        def turn_bd():
            for r in range(O // P):
                nc.tensor.matmul(out=gp[:, 4:5, r], lhsT=bg_rows[:, P * r : P * (r + 1)], rhs=pick[:, 4:5], start=True, stop=True)

        def copy_rows():
            nc.scalar.copy(out=halves[:, 0:4, :], in_=gp[:, 0:4, :])

        def copy_bd():
            nc.scalar.copy(out=halves[:, 4, :], in_=gp[:, 4, :])

        xw = {}
        xg = {}

        def widen(c, engine, a0=0, a1=V):
            if c not in xw:
                made = work.tile([P, V * D], BF16, name="xw", align_bytes=64, bufs=4)
                xw[c] = made
            cols = slice(D * a0, D * a1)
            src = xb[c][:].rearrange("q a k -> q (a k)")[:, cols].bitcast(FP8)
            nc.vector.tensor_copy(out=xw[c][:, cols], in_=src)

        def widen_scaled(c, a, engine):
            if c not in xw:
                made = work.tile([P, V * D], BF16, name="xw", align_bytes=64, bufs=4)
                xw[c] = made
            for j in range(4):
                cols = slice(D * a + P * j, D * a + P * (j + 1))
                at = 16 * a + 4 * c + j
                src = xb[c][:].rearrange("q a k -> q (a k)")[:, cols].bitcast(FP8)
                if engine == "v":
                    nc.vector.tensor_scalar(out=xw[c][:, cols], in0=src, scalar1=xs[:, at : at + 1], scalar2=None, op0=MULT)
                else:
                    nc.scalar.activation(out=xw[c][:, cols], in_=src, func=ACT.Copy, scale=xs[:, at : at + 1])

        def copy_x(c, engine, label):
            made = work.tile([P, V, P * T4], BF16, name=label, align_bytes=64, bufs=1)
            xg[c] = made
            dst = made[:].bitcast(F32).rearrange("q a (r u) -> q a r u", u=2)
            src = held["xtb", c][:].rearrange("q a u r -> q a r u")
            if engine == "v":
                nc.vector.tensor_copy(out=dst, in_=src)
            else:
                nc.scalar.copy(out=dst, in_=src)

        def copy_half(c, a, engine):
            if c not in xg:
                made = work.tile([P, V, P * T4], BF16, name="xg", align_bytes=64, bufs=4)
                xg[c] = made
            dst = xg[c][:, a, :].bitcast(F32).rearrange("q (r u) -> q r u", u=2)
            nc.vector.tensor_copy(out=dst, in_=held["xt", c, a].rearrange("q u r -> q r u"))

        def turn(c, a0=0, a1=V, pool=ps_proj, label="proj"):
            bank = pool.tile([P, a1 - a0, 2, P], F32, name=label)
            for a in range(a0, a1):
                words = xw[c][:, D * a : D * (a + 1)].bitcast(F32)
                for u in range(2):
                    nc.tensor.transpose(bank[:, a - a0, u, :], words[:, u : D // 2 : 2], ident[:])
                held["xt", c, a] = bank[:, a - a0, :, :]
            held["xtb", c] = bank

        def scale_out(c, a, engine):
            if c not in xg:
                made = work.tile([P, V, P * T4], BF16, name="xg", align_bytes=64, bufs=4)
                xg[c] = made
            src = held["xt", c, a].bitcast(BF16).rearrange("q u (r e) -> q r u e", e=2)
            dst = xg[c][:, a, :].rearrange("q (r u e) -> q r u e", u=2, e=2)
            at = V * 16 + 4 * a + c
            if engine == "v":
                nc.vector.tensor_scalar(out=dst, in0=src, scalar1=xs[:, at : at + 1], scalar2=None, op0=MULT)
            else:
                nc.scalar.activation(out=dst, in_=src, func=ACT.Copy, scale=xs[:, at : at + 1])

        xc = {}
        xsc = {}

        def quant_x(c, a0=0, a1=V):
            if a0 == 0:
                xc[c] = kept([P, N], U32, "xc%d" % c)
                xsc[c] = kept([P, N], U8, "xsc%d" % c)
            cols = slice(P * a0, P * a1)
            nc.vector.quantize_mx(
                out=xc[c][:, cols].bitcast(FP8X4), scales=xsc[c][:, cols], in_=xg[c][:, a0:a1, :].rearrange("q a n -> q (a n)")
            )

        pg = {}
        pc = {}
        psc = {}
        for w in range(2):
            pg[w] = kept([P, T4 * P * T4], BF16, "pg%d" % w)
            pc[w] = kept([P, H], U32, "pc%d" % w)
            psc[w] = kept([P, H], U8, "psc%d" % w)

        def lay_p(w, t0, engine, label="", count=2):
            dst = pg[w][:].rearrange("q (t m j) -> q t m j", t=T4, j=T4)[:, t0 : t0 + count]
            src = praw[w][:].rearrange("q j (m t) -> q t m j", t=T4)[:, t0 : t0 + count]
            if engine == "v":
                nc.vector.tensor_copy(
                    out=dst.rearrange("q t (m i) j -> q m t j i", i=2), in_=src.rearrange("q t (m i) j -> q m t j i", i=2)
                )

        def quant_p(w, t0, t1):
            cols = slice(P * t0, P * t1)
            nc.vector.quantize_mx(
                out=pc[w][:, cols].bitcast(FP8X4), scales=psc[w][:, cols], in_=pg[w][:, T4 * P * t0 : T4 * P * t1]
            )

        th = {}

        def project(c, w, t0):
            acc = ps_proj.tile([P, 2, N], F32, name="proj")
            for t in range(t0, t0 + 2):
                cols = slice(P * t, P * (t + 1))
                nc.tensor.matmul_mx(
                    out=acc[:, t - t0, :],
                    lhsT=pc[w][:, cols].bitcast(FP8X4),
                    lhsT_scale=psc[w][:, cols],
                    rhs=xc[c][:].bitcast(FP8X4),
                    rhs_scale=xsc[c][:],
                    start=True,
                    stop=True,
                )
            held["proj", c, w, t0] = acc

        def squash(c, w, t0):
            if t0 == 0:
                made = work.tile([P, T4, N], F32, name="th", bufs=8)
                th[c, w] = made
            acc = held["proj", c, w, t0]
            for t in range(t0, t0 + 2):
                nc.scalar.activation(
                    out=th[c, w][:, t, :], in_=acc[:, t - t0, :], func=ACT.Tanh, bias=halves[:, w, t : t + 1], scale=0.5
                )

        qg = {}

        def gain(c, w, engine, factor, n0=0, n1=N):
            if (c, w) not in qg:
                made = work.tile([P, N * T4], BF16, name="qg%d" % ((c + w) % 2), align_bytes=64, bufs=1)
                qg[c, w] = made
            run = 2 if factor is gp else 1
            engine.tensor_tensor(
                out=qg[c, w][:, T4 * n0 : T4 * n1].rearrange("q (n i t) -> q n t i", i=run, t=T4),
                in0=th[c, w][:, :, n0:n1].rearrange("q t (n i) -> q n t i", i=run),
                in1=factor[:, 2 + w, :].unsqueeze(1).unsqueeze(3).to_broadcast([P, (n1 - n0) // run, T4, run]),
                op=MULT,
            )

        qc = {}
        qs = {}

        def quant_q(c, w):
            if c not in qc:
                codes = work.tile([P, 2 * N], U32, name="qc", align_bytes=64, bufs=4)
                scales = work.tile([P, 2 * N], U8, name="qs", align_bytes=64, bufs=4)
                qc[c] = codes
                qs[c] = scales
            cols = slice(N * w, N * (w + 1))
            nc.vector.quantize_mx(out=qc[c][:, cols].bitcast(FP8X4), scales=qs[c][:, cols], in_=qg[c, w][:])

        def decode(c, j, label, pool=ps_dec, w0=0, w1=2):
            if w0 == 0:
                made = pool.tile([P, O], F32, name=label)
                held["dec", c, j] = made
            acc = held["dec", c, j]
            for w in range(w0, w1):
                at = N * w + P * PARTS[j][w]
                nc.tensor.matmul_mx(
                    out=acc[:],
                    lhsT=qc[c][:, at : at + P].bitcast(FP8X4),
                    lhsT_scale=qs[c][:, at : at + P],
                    rhs=wdw[:, w, :].bitcast(FP4X4),
                    rhs_scale=wds[:, w, :],
                    start=(w == 0),
                    stop=(w == 1),
                )

        zs = {}

        def add_bias(c, j):
            if (c, j // 2) not in zs:
                made = work.tile([P, 2, O], F32, name="z", bufs=8)
                zs[c, j // 2] = made
            nc.vector.tensor_tensor(out=zs[c, j // 2][:, j % 2, :], in0=held["dec", c, j][:], in1=bdt[:], op=ADD)

        def finish(c, j0, count):
            y = work.tile([P, count, O], F32, name="y", bufs=14)
            nc.scalar.activation(out=y[:, 0:count, :], in_=zs[c, j0 // 2][:, j0 % 2 : j0 % 2 + count, :], func=ACT.Sigmoid)
            nc.sync.dma_start(
                out=out[j0 : j0 + count, P * c : P * (c + 1), :].rearrange("j q o -> q j o"), in_=y[:, 0:count, :]
            )

        yt = {}

        def decode_turned(c, j, label, pool=ps_dec):
            acc = pool.tile([P, O // P, P], F32, name=label)
            held["dect", c, j] = acc
            for r in range(O // P):
                for w in range(2):
                    at = N * w + P * PARTS[j][w]
                    nc.tensor.matmul_mx(
                        out=acc[:, r, :],
                        lhsT=wdw[:, w, 2 * P * r : 2 * P * (r + 1)].bitcast(FP4X4),
                        lhsT_scale=wds[:, w, P * r : P * (r + 1)],
                        rhs=qc[c][:, at : at + P].bitcast(FP8X4),
                        rhs_scale=qs[c][:, at : at + P],
                        start=(w == 0),
                        stop=(w == 1),
                    )

        def finish_turned(c, j):
            yt[c, j] = kept([P, O // P, P], F32, "yt%d%d" % (c, j))
            for r in range(O // P):
                nc.scalar.activation(
                    out=yt[c, j][:, r, :], in_=held["dect", c, j][:, r, :], func=ACT.Sigmoid, bias=halves[:, 4, r : r + 1]
                )

        def turn_back(c, j, label, pool=ps_dec):
            bank = pool.tile([P, O], F32, name=label)
            held["back", c, j] = bank
            for r in range(O // P):
                nc.tensor.transpose(bank[:, P * r : P * (r + 1)], yt[c, j][:, r, :], ident[:])

        def store_turned(c, j):
            y = kept([P, O], F32, "turned%d%d" % (c, j))
            nc.scalar.copy(out=y[:], in_=held["back", c, j][:])
            nc.sync.dma_start(out=out[j, P * c : P * (c + 1), :], in_=y[:])

        warm_up("proj")
        spread_scales()
        widen(0, "v", 0, 1)
        widen(0, "v", 1, 2)
        turn(0, 0, 1, ps_dec, "dec1")
        turn(0, 1, 2, ps_dec, "dec2")
        turn_rows()
        warm_up("proj")
        lay_p(0, 0, "v")
        lay_p(0, 2, "v")
        scale_out(0, 0, "s")
        scale_out(0, 1, "s")
        copy_rows()
        widen_scaled(1, 0, "s")
        widen_scaled(1, 1, "s")
        quant_p(0, 0, 2)
        quant_x(0)
        quant_p(0, 2, 4)
        project(0, 0, 0)
        project(0, 0, 2)
        lay_p(1, 0, "v")
        lay_p(1, 2, "v")
        turn(1, 0, 2, ps_dec, "dec1")
        squash(0, 0, 0)
        copy_x(1, "s", "qg0")
        squash(0, 0, 2)
        quant_p(1, 0, 2)
        project(0, 1, 0)
        quant_p(1, 2, 4)
        project(0, 1, 2)
        widen(2, "v")
        turn(2, 0, 2, ps_dec, "dec2")
        quant_x(1)
        widen(3, "v")
        gain(0, 0, nc.gpsimd, gh, 0, SHARE)
        gain(0, 0, nc.vector, gp, SHARE, N)
        scale_out(2, 0, "v")
        scale_out(2, 1, "v")
        squash(0, 1, 0)
        project(1, 0, 0)
        squash(0, 1, 2)
        project(1, 0, 2)
        turn(3, 0, 2, ps_dec, "dec3")
        gain(0, 1, nc.vector, gp)
        scale_out(3, 0, "v")
        scale_out(3, 1, "v")
        squash(1, 0, 0)
        project(1, 1, 0)
        squash(1, 0, 2)
        project(1, 1, 2)
        turn_bd()
        quant_x(2)
        quant_x(3)
        quant_q(0, 1)
        quant_q(0, 0)
        gain(1, 0, nc.gpsimd, gh)
        squash(1, 1, 0)
        project(2, 0, 0)
        squash(1, 1, 2)
        copy_bd()
        project(2, 0, 2)
        project(2, 1, 0)
        decode(0, 0, "dec0")
        decode(0, 1, "dec1")
        gain(1, 1, nc.vector, gp)
        squash(2, 0, 0)
        project(2, 1, 2)
        decode(0, 2, "dec2")
        squash(2, 0, 2)
        project(3, 0, 0)
        decode(0, 3, "dec3")
        add_bias(0, 0)
        add_bias(0, 1)
        add_bias(0, 2)
        squash(2, 1, 0)
        project(3, 0, 2)
        squash(2, 1, 2)
        project(3, 1, 0)
        quant_q(1, 1)
        quant_q(1, 0)
        gain(2, 0, nc.gpsimd, gh)
        decode(1, 0, "dec0")
        decode(1, 1, "dec1")
        add_bias(0, 3)
        finish(0, 0, 2)
        squash(3, 0, 0)
        project(3, 1, 2)
        decode(1, 2, "dec2")
        decode_turned(1, 3, "dec3")
        gain(2, 1, nc.vector, gp)
        add_bias(1, 0)
        add_bias(1, 1)
        squash(3, 0, 2)
        finish(0, 2, 2)
        squash(3, 1, 0)
        squash(3, 1, 2)
        finish(1, 0, 2)
        finish_turned(1, 3)
        quant_q(2, 1)
        quant_q(2, 0)
        gain(3, 0, nc.gpsimd, gh)
        decode(2, 0, "dec0")
        decode(2, 1, "dec1")
        decode(2, 2, "proj", ps_proj)
        decode(2, 3, "proj", ps_proj)
        add_bias(1, 2)
        gain(3, 1, nc.vector, gp)
        finish(1, 2, 1)
        add_bias(2, 0)
        add_bias(2, 1)
        turn_back(1, 3, "dec3")
        finish(2, 0, 1)
        store_turned(1, 3)
        finish(2, 1, 1)
        quant_q(3, 1)
        quant_q(3, 0)
        decode(3, 0, "dec2")
        decode(3, 1, "dec0")
        decode(3, 2, "dec1")
        decode(3, 3, "dec3")
        add_bias(2, 2)
        add_bias(2, 3)
        finish(2, 2, 1)
        finish(2, 3, 1)
        for j in range(4):
            add_bias(3, j)
            finish(3, j, 1)
